import numpy as np
import ml_dtypes


def mxq(x, axis, fmt="e4m3"):
    dtype, down = {"e4m3": (ml_dtypes.float8_e4m3fn, 7), "e5m2": (ml_dtypes.float8_e5m2, 14)}[fmt]
    v = np.moveaxis(np.asarray(x, np.float32).astype(ml_dtypes.bfloat16).astype(np.float64), axis, -1)
    blocks = v.reshape(v.shape[:-1] + (-1, 32))
    amax = np.abs(blocks).max(-1, keepdims=True)
    byte = np.maximum(np.where(amax > 0, np.frexp(amax)[1] - 1 + 127, 0) - down, 1)
    scale = np.exp2(byte - 127.0)
    codes = (blocks / scale).astype(np.float32).astype(dtype).astype(np.float64)
    return np.moveaxis((codes * scale).reshape(v.shape), -1, axis)


WIDE = False


def mx_kscale(k):
    if not WIDE:
        return np.ones(k)
    levels = np.array([10, -10, 5, -5, 0])
    if k % 512:
        return np.exp2(np.random.permutation(np.resize(levels, k // 32))).repeat(32)
    a = np.empty((k // 512, 16))
    for p in range(k // 512):
        a[p, :8] = np.random.permutation(np.resize(levels, 8))
        for g in range(8):
            far = levels[np.abs(levels - a[p, g]) >= 10]
            a[p, g + 8] = far[np.random.randint(len(far))]
    return np.exp2(a.ravel()).repeat(32)


def f64(x):
    return np.asarray(x).astype(np.float64)


def striped(idx):
    return np.tile(idx.reshape(-1, 16).T, (8, 1)).astype(np.uint16)


def unstriped(offs):
    return offs[:16].T.reshape(-1).astype(np.int64)


def pack_weight(w):
    k, n = w.shape
    w = f64(np.asarray(w, np.float32).astype(ml_dtypes.bfloat16)).reshape(k // 32, 32, n)
    amax = np.abs(w).max(1)
    byte = np.clip(np.where(amax > 0, np.frexp(amax)[1] - 1 + 127 - 7, 1), 1, 254)
    scaled = (w * np.exp2(127.0 - byte)[:, None, :]).reshape(k, n).astype(np.float32)
    words = np.ascontiguousarray(scaled.reshape(k // 512, 128, 4, n).transpose(0, 1, 3, 2)).astype(ml_dtypes.float8_e4m3fn).view(np.uint8)
    return words, np.ascontiguousarray(byte.astype(np.uint8).reshape(k // 512, 16, n))


def unpack_weight(words, scales):
    g, p, n, _ = words.shape
    vals = np.ascontiguousarray(words).view(ml_dtypes.float8_e4m3fn).astype(np.float64) * np.repeat(np.exp2(scales.astype(np.float64) - 127.0), 8, axis=1)[..., None]
    return vals.transpose(0, 1, 3, 2).reshape(g * 512, n)


E2M1 = np.array([0.0, 0.5, 1.0, 1.5, 2.0, 3.0, 4.0, 6.0, -0.0, -0.5, -1.0, -1.5, -2.0, -3.0, -4.0, -6.0])


def pack_fp4(w):
    k, n = w.shape
    w = f64(np.asarray(w, np.float32).astype(ml_dtypes.bfloat16)).reshape(k // 32, 32, n)
    amax = np.abs(w).max(1)
    mant, ex = np.frexp(amax / 6.0)
    byte = np.clip(np.where(amax > 0, np.where(mant > 0.5, ex, ex - 1) + 127, 1), 1, 254)
    scaled = (w * np.exp2(127.0 - byte)[:, None, :]).reshape(k, n).astype(np.float32)
    c = np.ascontiguousarray(scaled.reshape(k // 512, 128, 4, n).transpose(0, 1, 3, 2)).astype(ml_dtypes.float4_e2m1fn).view(np.uint8) & 0xF
    words = (c[..., 0::2] | (c[..., 1::2] << 4)).reshape(k // 512, 128, 2 * n)
    return np.ascontiguousarray(words), np.ascontiguousarray(byte.astype(np.uint8).reshape(k // 512, 16, n))


def unpack_fp4(words, scales):
    g, _, n = scales.shape
    words = np.ascontiguousarray(words).reshape(g, 128, n, 2)
    nib = np.empty((g, 128, n, 4), np.uint8)
    nib[..., 0::2] = words & 0xF
    nib[..., 1::2] = words >> 4
    vals = E2M1[nib] * np.repeat(np.exp2(scales.astype(np.float64) - 127.0), 8, axis=1)[..., None]
    return vals.transpose(0, 1, 3, 2).reshape(g * 512, n)


def relu(v):
    return np.maximum(v, 0.0)


K, T, S, H, N = 512, 4096, 1024, 512, 256


def setup_inputs():
    n = np.random.standard_normal
    s = mx_kscale(K)[:, None]
    u = mx_kscale(H)
    packed_xT = pack_weight(n((K, T)) * s)
    packed_w1 = pack_fp4(n((K, N)) / np.sqrt(2 * K) / s)
    packed_w3 = pack_fp4(n((H, N)) / np.sqrt(2 * H) / u[:, None])
    return {
        "x_words": packed_xT[0],
        "x_scales": packed_xT[1],
        "w1_words": packed_w1[0],
        "w1_scales": packed_w1[1],
        "w2": (n((K, H)) / np.sqrt(K) / s * u).astype(np.float32),
        "w3_words": packed_w3[0],
        "w3_scales": packed_w3[1],
        "offs": striped(np.random.permutation(T)[:S]),
    }


def reference(x_words, x_scales, w1_words, w1_scales, w2, w3_words, w3_scales, offs):
    xq = unpack_weight(x_words, x_scales)[:, unstriped(offs)]
    h = relu(mxq(f64(w2), 0, "e4m3").T @ xq)
    return unpack_fp4(w1_words, w1_scales).T @ xq + unpack_fp4(w3_words, w3_scales).T @ mxq(h, 0, "e4m3")

@@ -1,0 +1,185 @@
+from contextlib import ExitStack
+
+import concourse.mybir as mybir
+
+K, T, S, H, N = 512, 4096, 1024, 512, 256
+FLOPS = 2 * K * H * S + 2 * K * N * S + 2 * H * N * S
+
+F32 = mybir.dt.float32
+BF16 = mybir.dt.bfloat16
+I32 = mybir.dt.int32
+U32 = mybir.dt.uint32
+U16 = mybir.dt.uint16
+U8 = mybir.dt.uint8
+FP8X4 = mybir.dt.float8_e4m3fn_x4
+FP4X4 = mybir.dt.float4_e2m1fn_x4
+RELU = mybir.ActivationFunctionType.Relu
+COPY = mybir.ActivationFunctionType.Copy
+
+P = 128
+PACK = 4
+CHUNK = 128
+CHUNKS = S // CHUNK
+GATHER = 512
+M_TILES = N // P
+HALF = H // 2
+HALF_M = HALF // PACK
+LAG = 4
+PIECES = ((0, 2), (2, 2), (4, 2), (6, 1), (7, 1))
+
+
+def tile_picked_lora_relu_p_kernel(
+    tc, x_words, x_scales, w1_words, w1_scales, w2, w3_words, w3_scales, offs, out
+):
+    nc = tc.nc
+    with ExitStack() as ctx:
+        keep = ctx.enter_context(tc.tile_pool(name="keep", bufs=1))
+        out_psum = ctx.enter_context(tc.psum_pool(name="out_psum", bufs=1))
+        h_psum = ctx.enter_context(tc.psum_pool(name="h_psum", bufs=3))
+
+        offsets = keep.tile([P, S // 16], U16, name="offsets")
+        nc.sync.dma_start(offsets[:], offs)
+        x_table = keep.tile([P, T], U32, name="x_table", align_bytes=64)
+        nc.sync.dma_start(x_table[:].bitcast(I32), x_words[0].rearrange("p c r -> p (c r)").bitcast(I32))
+        w2_rows = w2.rearrange("(p j) c -> p j c", j=PACK)
+        w2_raw = []
+        for half in range(2):
+            raw = keep.tile([P, PACK, HALF], F32, name="w2_raw%d" % half, align_bytes=64)
+            nc.sync.dma_start(raw[:], w2_rows[:, :, half * HALF : (half + 1) * HALF])
+            w2_raw.append(raw)
+
+        scale_table = keep.tile([P, T], U8, name="scale_table", align_bytes=64)
+        nc.vector.memset(scale_table[:].bitcast(I32), 0)
+        nc.scalar.dma_start(scale_table[4:P:8, :].bitcast(I32), x_scales[0].bitcast(I32))
+        x_scale = keep.tile([P, S], U8, name="x_scale", align_bytes=64)
+        nc.vector.memset(x_scale[:].bitcast(I32), 0)
+
+        packed = []
+        for name, words, scales in (("w1", w1_words, w1_scales), ("w3", w3_words, w3_scales)):
+            codes = keep.tile([P, 2 * N], U8, name=name + "_codes", align_bytes=64)
+            plane = keep.tile([P, N], U8, name=name + "_scale", align_bytes=64)
+            nc.gpsimd.memset(plane[:].bitcast(I32), 0)
+            nc.gpsimd.dma_start(codes[:].bitcast(I32), words[0].bitcast(I32))
+            for q in range(4):
+                nc.gpsimd.dma_start(
+                    plane[32 * q : 32 * q + 4, :].bitcast(I32), scales[0, 4 * q : 4 * q + 4, :].bitcast(I32)
+                )
+            packed.append((codes, plane))
+        (w1_codes, w1_scale), (w3_codes, w3_scale) = packed
+
+        scale_picked = keep.tile([P, S], U8, name="scale_picked", align_bytes=64)
+        nc.vector.tensor_copy(scale_picked[:], scale_table[:].indirect(offsets[:]))
+        for r in range(4):
+            nc.scalar.dma_start(x_scale[r:P:32, :].bitcast(I32), scale_picked[4 + 8 * r : P : 32, :].bitcast(I32))
+
+        x_codes = []
+        for g in range(S // GATHER):
+            picked = keep.tile([P, GATHER], U32, name="x_codes%d" % g, align_bytes=64)
+            columns = GATHER // 16
+            nc.vector.tensor_copy(picked[:], x_table[:].indirect(offsets[:, g * columns : (g + 1) * columns]))
+            x_codes.append(picked)
+
+        def x_operand(c):
+            g, first = divmod(c * CHUNK, GATHER)
+            return x_codes[g][:, first : first + CHUNK].bitcast(FP8X4), x_scale[:, c * CHUNK : (c + 1) * CHUNK]
+
+        def out_pass(bank, slot, codes, plane, rhs, rhs_scale, start, stop):
+            for mt in range(M_TILES):
+                nc.tensor.matmul_mx(
+                    out=bank[:, mt, slot * CHUNK : (slot + 1) * CHUNK],
+                    lhsT=codes[:, 2 * P * mt : 2 * P * (mt + 1)].bitcast(FP4X4),
+                    lhsT_scale=plane[:, P * mt : P * (mt + 1)],
+                    rhs=rhs,
+                    rhs_scale=rhs_scale,
+                    start=start and mt == 0,
+                    stop=stop and mt == M_TILES - 1,
+                )
+
+        out_banks = []
+        for first, count in PIECES:
+            bank = out_psum.tile([P, M_TILES, count * CHUNK], F32, name="out_bank%d" % first)
+            for slot in range(count):
+                rhs, rhs_scale = x_operand(first + slot)
+                out_pass(bank, slot, w1_codes, w1_scale, rhs, rhs_scale, slot == 0, False)
+            out_banks.append(bank)
+
+        w2_codes = keep.tile([P, H], U32, name="w2_codes", align_bytes=64)
+        w2_scale = keep.tile([P, H], U8, name="w2_scale", align_bytes=64)
+        grouped = []
+        for half in range(2):
+            tile = keep.tile([P, PACK, HALF_M, PACK], BF16, name="w2_grouped%d" % half, align_bytes=64)
+            src = w2_raw[half][:].rearrange("p j (m t) -> p m j t", t=PACK)
+            dst = tile[:].rearrange("p t m j -> p m j t")
+            if half == 0:
+                nc.scalar.activation(dst, src, COPY)
+            else:
+                nc.vector.tensor_copy(dst, src)
+            grouped.append(tile)
+        for half in range(2):
+            for t in range(PACK):
+                cols = slice(t * P + half * HALF_M, t * P + (half + 1) * HALF_M)
+                nc.vector.quantize_mx(
+                    out=w2_codes[:, cols].bitcast(FP8X4),
+                    scales=w2_scale[:, cols],
+                    in_=grouped[half][:, t, :, :].rearrange("p m j -> p (m j)"),
+                )
+
+        hidden = {}
+
+        def first_product(c):
+            bank = h_psum.tile([P, PACK, CHUNK], F32, name="h_bank")
+            rhs, rhs_scale = x_operand(c)
+            for t in range(PACK):
+                nc.tensor.matmul_mx(
+                    out=bank[:, t, :],
+                    lhsT=w2_codes[:, t * P : (t + 1) * P].bitcast(FP8X4),
+                    lhsT_scale=w2_scale[:, t * P : (t + 1) * P],
+                    rhs=rhs,
+                    rhs_scale=rhs_scale,
+                    start=True,
+                    stop=True,
+                )
+            h = keep.tile([P, CHUNK, PACK], BF16, name="h%d" % c, align_bytes=64)
+            src = bank[:].rearrange("p t n -> p n t")
+            if c % 2 == 0:
+                nc.scalar.activation(h[:], src, RELU)
+            else:
+                nc.vector.tensor_scalar_max(h[:], src, 0.0)
+            hidden[c] = h
+
+        out_view = out.rearrange("(mt p) s -> p mt s", p=P)
+
+        quantised = {}
+
+        def quantise_hidden(c):
+            h_codes = keep.tile([P, CHUNK], U32, name="h_codes%d" % c, align_bytes=64)
+            h_scale = keep.tile([P, CHUNK], U8, name="h_scale%d" % c, align_bytes=64)
+            nc.vector.quantize_mx(
+                out=h_codes[:].bitcast(FP8X4), scales=h_scale[:], in_=hidden[c][:].rearrange("p n t -> p (n t)")
+            )
+            quantised[c] = (h_codes, h_scale)
+
+        def second_product(c):
+            h_codes, h_scale = quantised[c]
+            for piece, (first, count) in enumerate(PIECES):
+                if first <= c < first + count:
+                    last = c == first + count - 1
+                    bank = out_banks[piece]
+                    out_pass(bank, c - first, w3_codes, w3_scale, h_codes[:].bitcast(FP8X4), h_scale[:], False, last)
+                    if last:
+                        staged = keep.tile([P, M_TILES, count * CHUNK], F32, name="staged%d" % first)
+                        if piece == len(PIECES) - 1:
+                            nc.vector.tensor_copy(staged[:], bank[:])
+                        else:
+                            nc.scalar.copy(staged[:], bank[:])
+                        nc.sync.dma_start(out_view[:, :, first * CHUNK : (first + count) * CHUNK], staged[:])
+
+        for step in range(CHUNKS + LAG):
+            if step < CHUNKS:
+                first_product(step)
+                if step % 2 == 1:
+                    quantise_hidden(step - 1)
+                    quantise_hidden(step)
+            if step >= LAG and step % 2 == 0:
+                second_product(step - LAG)
+                second_product(step - LAG + 1)

@@ -35,7 +35,7 @@ def tile_picked_lora_relu_p_kernel(
     with ExitStack() as ctx:
         keep = ctx.enter_context(tc.tile_pool(name="keep", bufs=1))
         out_psum = ctx.enter_context(tc.psum_pool(name="out_psum", bufs=1))
-        h_psum = ctx.enter_context(tc.psum_pool(name="h_psum", bufs=3))
+        h_psum = ctx.enter_context(tc.psum_pool(name="h_psum", bufs=4))
 
         offsets = keep.tile([P, S // 16], U16, name="offsets")
         nc.sync.dma_start(offsets[:], offs)
@@ -48,33 +48,36 @@ def tile_picked_lora_relu_p_kernel(
             nc.sync.dma_start(raw[:], w2_rows[:, :, half * HALF : (half + 1) * HALF])
             w2_raw.append(raw)
 
-        scale_table = keep.tile([P, T], U8, name="scale_table", align_bytes=64)
+        scale_table = keep.tile([P, T], U8, name="scale_table", tag="table", align_bytes=64)
         nc.vector.memset(scale_table[:].bitcast(I32), 0)
         nc.scalar.dma_start(scale_table[4:P:8, :].bitcast(I32), x_scales[0].bitcast(I32))
         x_scale = keep.tile([P, S], U8, name="x_scale", align_bytes=64)
         nc.vector.memset(x_scale[:].bitcast(I32), 0)
 
-        packed = []
-        for name, words, scales in (("w1", w1_words, w1_scales), ("w3", w3_words, w3_scales)):
-            codes = keep.tile([P, 2 * N], U8, name=name + "_codes", align_bytes=64)
-            plane = keep.tile([P, N], U8, name=name + "_scale", align_bytes=64)
-            nc.gpsimd.memset(plane[:].bitcast(I32), 0)
-            nc.gpsimd.dma_start(codes[:].bitcast(I32), words[0].bitcast(I32))
+        def load_scale_rows(queue, plane, scales):
+            nc.gpsimd.memset(plane.bitcast(I32), 0)
             for q in range(4):
-                nc.gpsimd.dma_start(
-                    plane[32 * q : 32 * q + 4, :].bitcast(I32), scales[0, 4 * q : 4 * q + 4, :].bitcast(I32)
-                )
-            packed.append((codes, plane))
-        (w1_codes, w1_scale), (w3_codes, w3_scale) = packed
+                queue.dma_start(plane[32 * q : 32 * q + 4, :].bitcast(I32), scales[0, 4 * q : 4 * q + 4, :].bitcast(I32))
 
-        scale_picked = keep.tile([P, S], U8, name="scale_picked", align_bytes=64)
+        w1_codes = keep.tile([P, 2 * N], U8, name="w1_codes", align_bytes=64)
+        nc.scalar.dma_start(w1_codes[:].bitcast(I32), w1_words[0].bitcast(I32))
+        w1_scale = keep.tile([P, N], U8, name="w1_scale", align_bytes=64)
+        load_scale_rows(nc.gpsimd, w1_scale[:], w1_scales)
+
+        scale_picked = keep.tile([P, S], U8, name="scale_picked", tag="picked", align_bytes=64)
         nc.vector.tensor_copy(scale_picked[:], scale_table[:].indirect(offsets[:]))
         for r in range(4):
             nc.scalar.dma_start(x_scale[r:P:32, :].bitcast(I32), scale_picked[4 + 8 * r : P : 32, :].bitcast(I32))
 
+        w3_tile = keep.tile([P, 3 * N], U8, name="w3_tile", tag="picked", align_bytes=64)
+        w3_codes = w3_tile[:, : 2 * N]
+        w3_scale = w3_tile[:, 2 * N :]
+        nc.sync.dma_start(w3_codes.bitcast(I32), w3_words[0].bitcast(I32))
+        load_scale_rows(nc.sync, w3_scale, w3_scales)
+
         x_codes = []
         for g in range(S // GATHER):
-            picked = keep.tile([P, GATHER], U32, name="x_codes%d" % g, align_bytes=64)
+            picked = keep.tile([P, GATHER], U32, name="x_codes%d" % g, tag="table" if g == 0 else "second", align_bytes=64)
             columns = GATHER // 16
             nc.vector.tensor_copy(picked[:], x_table[:].indirect(offsets[:, g * columns : (g + 1) * columns]))
             x_codes.append(picked)
@@ -96,12 +99,15 @@ def tile_picked_lora_relu_p_kernel(
                 )
 
         out_banks = []
-        for first, count in PIECES:
-            bank = out_psum.tile([P, M_TILES, count * CHUNK], F32, name="out_bank%d" % first)
+
+        def open_piece(bank, first, count):
             for slot in range(count):
                 rhs, rhs_scale = x_operand(first + slot)
                 out_pass(bank, slot, w1_codes, w1_scale, rhs, rhs_scale, slot == 0, False)
             out_banks.append(bank)
+
+        for first, count in PIECES[:-1]:
+            open_piece(out_psum.tile([P, M_TILES, count * CHUNK], F32, name="out_bank%d" % first), first, count)
 
         w2_codes = keep.tile([P, H], U32, name="w2_codes", align_bytes=64)
         w2_scale = keep.tile([P, H], U8, name="w2_scale", align_bytes=64)
@@ -168,7 +174,7 @@ def tile_picked_lora_relu_p_kernel(
                     out_pass(bank, c - first, w3_codes, w3_scale, h_codes[:].bitcast(FP8X4), h_scale[:], False, last)
                     if last:
                         staged = keep.tile([P, M_TILES, count * CHUNK], F32, name="staged%d" % first)
-                        if piece == len(PIECES) - 1:
+                        if count == 1:
                             nc.vector.tensor_copy(staged[:], bank[:])
                         else:
                             nc.scalar.copy(staged[:], bank[:])
@@ -180,6 +186,9 @@ def tile_picked_lora_relu_p_kernel(
                 if step % 2 == 1:
                     quantise_hidden(step - 1)
                     quantise_hidden(step)
+            if step == CHUNKS:
+                first, count = PIECES[-1]
+                open_piece(h_psum.tile([P, M_TILES, count * CHUNK], F32, name="h_bank"), first, count)
             if step >= LAG and step % 2 == 0:
                 second_product(step - LAG)
                 second_product(step - LAG + 1)

@@ -25,6 +25,9 @@ M_TILES = N // P
 HALF = H // 2
 HALF_M = HALF // PACK
 LAG = 4
+EARLY = 4
+X_FIRST = 1536
+VECTOR_M = 44
 PIECES = ((0, 2), (2, 2), (4, 2), (6, 1), (7, 1))
 
 
@@ -39,45 +42,48 @@ def tile_picked_lora_relu_p_kernel(
 
         offsets = keep.tile([P, S // 16], U16, name="offsets")
         nc.sync.dma_start(offsets[:], offs)
-        x_table = keep.tile([P, T], U32, name="x_table", align_bytes=64)
-        nc.sync.dma_start(x_table[:].bitcast(I32), x_words[0].rearrange("p c r -> p (c r)").bitcast(I32))
-        w2_rows = w2.rearrange("(p j) c -> p j c", j=PACK)
-        w2_raw = []
-        for half in range(2):
-            raw = keep.tile([P, PACK, HALF], F32, name="w2_raw%d" % half, align_bytes=64)
-            nc.sync.dma_start(raw[:], w2_rows[:, :, half * HALF : (half + 1) * HALF])
-            w2_raw.append(raw)
-
-        scale_table = keep.tile([P, T], U8, name="scale_table", tag="table", align_bytes=64)
-        nc.vector.memset(scale_table[:].bitcast(I32), 0)
-        nc.scalar.dma_start(scale_table[4:P:8, :].bitcast(I32), x_scales[0].bitcast(I32))
-        x_scale = keep.tile([P, S], U8, name="x_scale", align_bytes=64)
-        nc.vector.memset(x_scale[:].bitcast(I32), 0)
-
         def load_scale_rows(queue, plane, scales):
-            nc.gpsimd.memset(plane.bitcast(I32), 0)
             for q in range(4):
                 queue.dma_start(plane[32 * q : 32 * q + 4, :].bitcast(I32), scales[0, 4 * q : 4 * q + 4, :].bitcast(I32))
 
-        w1_codes = keep.tile([P, 2 * N], U8, name="w1_codes", align_bytes=64)
-        nc.scalar.dma_start(w1_codes[:].bitcast(I32), w1_words[0].bitcast(I32))
+        x_table = keep.tile([P, T], U32, name="x_table", align_bytes=64)
+        x_rows = x_words[0].rearrange("p c r -> p (c r)").bitcast(I32)
+        scale_table = keep.tile([P, T], U8, name="scale_table", tag="table", align_bytes=64)
+        nc.vector.memset(scale_table[:].bitcast(I32), 0)
         w1_scale = keep.tile([P, N], U8, name="w1_scale", align_bytes=64)
-        load_scale_rows(nc.gpsimd, w1_scale[:], w1_scales)
+        nc.vector.memset(w1_scale[:].bitcast(I32), 0)
+        nc.sync.dma_start(x_table[:, :X_FIRST].bitcast(I32), x_rows[:, :X_FIRST])
+        load_scale_rows(nc.sync, scale_table[:], x_scales)
+        nc.sync.dma_start(x_table[:, X_FIRST:].bitcast(I32), x_rows[:, X_FIRST:])
 
-        scale_picked = keep.tile([P, S], U8, name="scale_picked", tag="picked", align_bytes=64)
-        nc.vector.tensor_copy(scale_picked[:], scale_table[:].indirect(offsets[:]))
-        for r in range(4):
-            nc.scalar.dma_start(x_scale[r:P:32, :].bitcast(I32), scale_picked[4 + 8 * r : P : 32, :].bitcast(I32))
+        w1_codes = keep.tile([P, 2 * N], U8, name="w1_codes", align_bytes=64)
+        nc.sync.dma_start(w1_codes[:].bitcast(I32), w1_words[0].bitcast(I32))
+        load_scale_rows(nc.sync, w1_scale[:], w1_scales)
 
-        w3_tile = keep.tile([P, 3 * N], U8, name="w3_tile", tag="picked", align_bytes=64)
+        w2_rows = w2.rearrange("(p j) c -> p j c", j=PACK)
+        w2_raw = []
+
+        def load_w2_half(half, tag):
+            raw = keep.tile([P, PACK, HALF], F32, name="w2_raw%d" % half, tag=tag, align_bytes=64)
+            nc.sync.dma_start(raw[:], w2_rows[:, :, half * HALF : (half + 1) * HALF])
+            w2_raw.append(raw)
+
+        load_w2_half(0, "w2_first")
+        load_w2_half(1, "w2_second")
+
+        x_scale = keep.tile([P, S], U8, name="x_scale", align_bytes=64)
+        nc.vector.tensor_copy(x_scale[:], scale_table[:].indirect(offsets[:]))
+
+        w3_tile = keep.tile([P, 3 * N], U8, name="w3_tile", tag="table", align_bytes=64)
         w3_codes = w3_tile[:, : 2 * N]
         w3_scale = w3_tile[:, 2 * N :]
         nc.sync.dma_start(w3_codes.bitcast(I32), w3_words[0].bitcast(I32))
+        nc.vector.memset(w3_scale.bitcast(I32), 0)
         load_scale_rows(nc.sync, w3_scale, w3_scales)
 
         x_codes = []
         for g in range(S // GATHER):
-            picked = keep.tile([P, GATHER], U32, name="x_codes%d" % g, tag="table" if g == 0 else "second", align_bytes=64)
+            picked = keep.tile([P, GATHER], U32, name="x_codes%d" % g, align_bytes=64)
             columns = GATHER // 16
             nc.vector.tensor_copy(picked[:], x_table[:].indirect(offsets[:, g * columns : (g + 1) * columns]))
             x_codes.append(picked)
@@ -106,7 +112,7 @@ def tile_picked_lora_relu_p_kernel(
                 out_pass(bank, slot, w1_codes, w1_scale, rhs, rhs_scale, slot == 0, False)
             out_banks.append(bank)
 
-        for first, count in PIECES[:-1]:
+        for first, count in PIECES[:EARLY]:
             open_piece(out_psum.tile([P, M_TILES, count * CHUNK], F32, name="out_bank%d" % first), first, count)
 
         w2_codes = keep.tile([P, H], U32, name="w2_codes", align_bytes=64)
@@ -119,7 +125,8 @@ def tile_picked_lora_relu_p_kernel(
             if half == 0:
                 nc.scalar.activation(dst, src, COPY)
             else:
-                nc.vector.tensor_copy(dst, src)
+                nc.vector.tensor_copy(dst[:, :VECTOR_M], src[:, :VECTOR_M])
+                nc.scalar.activation(dst[:, VECTOR_M:], src[:, VECTOR_M:], COPY)
             grouped.append(tile)
         for half in range(2):
             for t in range(PACK):
@@ -187,8 +194,8 @@ def tile_picked_lora_relu_p_kernel(
                     quantise_hidden(step - 1)
                     quantise_hidden(step)
             if step == CHUNKS:
-                first, count = PIECES[-1]
-                open_piece(h_psum.tile([P, M_TILES, count * CHUNK], F32, name="h_bank"), first, count)
+                for first, count in PIECES[EARLY:]:
+                    open_piece(h_psum.tile([P, M_TILES, count * CHUNK], F32, name="h_bank"), first, count)
             if step >= LAG and step % 2 == 0:
                 second_product(step - LAG)
                 second_product(step - LAG + 1)

@@ -28,7 +28,8 @@ LAG = 4
 EARLY = 4
 X_FIRST = 1536
 VECTOR_M = 44
-PIECES = ((0, 2), (2, 2), (4, 2), (6, 1), (7, 1))
+PIECES = ((0, (0, 1)), (2, (0, 1)), (4, (0, 1)), (6, (0,)), (6, (1,)))
+PAIR = 2
 
 
 def tile_picked_lora_relu_p_kernel(
@@ -42,9 +43,10 @@ def tile_picked_lora_relu_p_kernel(
 
         offsets = keep.tile([P, S // 16], U16, name="offsets")
         nc.sync.dma_start(offsets[:], offs)
-        def load_scale_rows(queue, plane, scales):
-            for q in range(4):
-                queue.dma_start(plane[32 * q : 32 * q + 4, :].bitcast(I32), scales[0, 4 * q : 4 * q + 4, :].bitcast(I32))
+
+        def load_scale_rows(plane, rows):
+            for r in range(4):
+                nc.sync.dma_start(plane[r:P:32, :].bitcast(I32), rows[r:16:4, :].bitcast(I32))
 
         x_table = keep.tile([P, T], U32, name="x_table", align_bytes=64)
         x_rows = x_words[0].rearrange("p c r -> p (c r)").bitcast(I32)
@@ -53,12 +55,12 @@ def tile_picked_lora_relu_p_kernel(
         w1_scale = keep.tile([P, N], U8, name="w1_scale", align_bytes=64)
         nc.vector.memset(w1_scale[:].bitcast(I32), 0)
         nc.sync.dma_start(x_table[:, :X_FIRST].bitcast(I32), x_rows[:, :X_FIRST])
-        load_scale_rows(nc.sync, scale_table[:], x_scales)
+        load_scale_rows(scale_table[:], x_scales[0])
         nc.sync.dma_start(x_table[:, X_FIRST:].bitcast(I32), x_rows[:, X_FIRST:])
 
         w1_codes = keep.tile([P, 2 * N], U8, name="w1_codes", align_bytes=64)
         nc.sync.dma_start(w1_codes[:].bitcast(I32), w1_words[0].bitcast(I32))
-        load_scale_rows(nc.sync, w1_scale[:], w1_scales)
+        load_scale_rows(w1_scale[:], w1_scales[0])
 
         w2_rows = w2.rearrange("(p j) c -> p j c", j=PACK)
         w2_raw = []
@@ -79,7 +81,7 @@ def tile_picked_lora_relu_p_kernel(
         w3_scale = w3_tile[:, 2 * N :]
         nc.sync.dma_start(w3_codes.bitcast(I32), w3_words[0].bitcast(I32))
         nc.vector.memset(w3_scale.bitcast(I32), 0)
-        load_scale_rows(nc.sync, w3_scale, w3_scales)
+        load_scale_rows(w3_scale, w3_scales[0])
 
         x_codes = []
         for g in range(S // GATHER):
@@ -92,28 +94,29 @@ def tile_picked_lora_relu_p_kernel(
             g, first = divmod(c * CHUNK, GATHER)
             return x_codes[g][:, first : first + CHUNK].bitcast(FP8X4), x_scale[:, c * CHUNK : (c + 1) * CHUNK]
 
-        def out_pass(bank, slot, codes, plane, rhs, rhs_scale, start, stop):
-            for mt in range(M_TILES):
+        def out_pass(bank, slot, m_tiles, codes, plane, rhs, rhs_scale, start, stop):
+            for place, mt in enumerate(m_tiles):
                 nc.tensor.matmul_mx(
-                    out=bank[:, mt, slot * CHUNK : (slot + 1) * CHUNK],
+                    out=bank[:, place, slot * CHUNK : (slot + 1) * CHUNK],
                     lhsT=codes[:, 2 * P * mt : 2 * P * (mt + 1)].bitcast(FP4X4),
                     lhsT_scale=plane[:, P * mt : P * (mt + 1)],
                     rhs=rhs,
                     rhs_scale=rhs_scale,
-                    start=start and mt == 0,
-                    stop=stop and mt == M_TILES - 1,
+                    start=start and place == 0,
+                    stop=stop and place == len(m_tiles) - 1,
                 )
 
         out_banks = []
 
-        def open_piece(bank, first, count):
-            for slot in range(count):
+        def open_piece(pool, name, first, m_tiles):
+            bank = pool.tile([P, len(m_tiles), PAIR * CHUNK], F32, name=name)
+            for slot in range(PAIR):
                 rhs, rhs_scale = x_operand(first + slot)
-                out_pass(bank, slot, w1_codes, w1_scale, rhs, rhs_scale, slot == 0, False)
+                out_pass(bank, slot, m_tiles, w1_codes, w1_scale, rhs, rhs_scale, slot == 0, False)
             out_banks.append(bank)
 
-        for first, count in PIECES[:EARLY]:
-            open_piece(out_psum.tile([P, M_TILES, count * CHUNK], F32, name="out_bank%d" % first), first, count)
+        for piece, (first, m_tiles) in enumerate(PIECES[:EARLY]):
+            open_piece(out_psum, "out_bank%d" % piece, first, m_tiles)
 
         w2_codes = keep.tile([P, H], U32, name="w2_codes", align_bytes=64)
         w2_scale = keep.tile([P, H], U8, name="w2_scale", align_bytes=64)
@@ -174,18 +177,20 @@ def tile_picked_lora_relu_p_kernel(
 
         def second_product(c):
             h_codes, h_scale = quantised[c]
-            for piece, (first, count) in enumerate(PIECES):
-                if first <= c < first + count:
-                    last = c == first + count - 1
+            for piece, (first, m_tiles) in enumerate(PIECES):
+                if first <= c < first + PAIR:
+                    last = c == first + PAIR - 1
                     bank = out_banks[piece]
-                    out_pass(bank, c - first, w3_codes, w3_scale, h_codes[:].bitcast(FP8X4), h_scale[:], False, last)
+                    out_pass(bank, c - first, m_tiles, w3_codes, w3_scale, h_codes[:].bitcast(FP8X4), h_scale[:], False, last)
                     if last:
-                        staged = keep.tile([P, M_TILES, count * CHUNK], F32, name="staged%d" % first)
-                        if count == 1:
+                        staged = keep.tile([P, len(m_tiles), PAIR * CHUNK], F32, name="staged%d" % piece)
+                        if piece == len(PIECES) - 1:
                             nc.vector.tensor_copy(staged[:], bank[:])
                         else:
                             nc.scalar.copy(staged[:], bank[:])
-                        nc.sync.dma_start(out_view[:, :, first * CHUNK : (first + count) * CHUNK], staged[:])
+                        nc.sync.dma_start(
+                            out_view[:, m_tiles[0] : m_tiles[-1] + 1, first * CHUNK : (first + PAIR) * CHUNK], staged[:]
+                        )
 
         for step in range(CHUNKS + LAG):
             if step < CHUNKS:
@@ -194,8 +199,8 @@ def tile_picked_lora_relu_p_kernel(
                     quantise_hidden(step - 1)
                     quantise_hidden(step)
             if step == CHUNKS:
-                for first, count in PIECES[EARLY:]:
-                    open_piece(h_psum.tile([P, M_TILES, count * CHUNK], F32, name="h_bank"), first, count)
+                for first, m_tiles in PIECES[EARLY:]:
+                    open_piece(h_psum, "h_bank", first, m_tiles)
             if step >= LAG and step % 2 == 0:
                 second_product(step - LAG)
                 second_product(step - LAG + 1)

@@ -26,8 +26,8 @@ HALF = H // 2
 HALF_M = HALF // PACK
 LAG = 4
 EARLY = 4
-X_FIRST = 1536
-VECTOR_M = 44
+X_FIRST = 2048
+VECTOR_M = 40
 PIECES = ((0, (0, 1)), (2, (0, 1)), (4, (0, 1)), (6, (0,)), (6, (1,)))
 PAIR = 2
 
@@ -38,6 +38,7 @@ def tile_picked_lora_relu_p_kernel(
     nc = tc.nc
     with ExitStack() as ctx:
         keep = ctx.enter_context(tc.tile_pool(name="keep", bufs=1))
+        reused = ctx.enter_context(tc.tile_pool(name="reused", bufs=1))
         out_psum = ctx.enter_context(tc.psum_pool(name="out_psum", bufs=1))
         h_psum = ctx.enter_context(tc.psum_pool(name="h_psum", bufs=4))
 
@@ -48,39 +49,39 @@ def tile_picked_lora_relu_p_kernel(
             for r in range(4):
                 nc.sync.dma_start(plane[r:P:32, :].bitcast(I32), rows[r:16:4, :].bitcast(I32))
 
+        scale_table = reused.tile([P, T], U8, name="scale_table", align_bytes=64, offset=0)
+        nc.sync.dma_start(scale_table[P - 16 :, :].bitcast(I32), x_scales[0].bitcast(I32))
         x_table = keep.tile([P, T], U32, name="x_table", align_bytes=64)
         x_rows = x_words[0].rearrange("p c r -> p (c r)").bitcast(I32)
-        scale_table = keep.tile([P, T], U8, name="scale_table", tag="table", align_bytes=64)
-        nc.vector.memset(scale_table[:].bitcast(I32), 0)
-        w1_scale = keep.tile([P, N], U8, name="w1_scale", align_bytes=64)
-        nc.vector.memset(w1_scale[:].bitcast(I32), 0)
         nc.sync.dma_start(x_table[:, :X_FIRST].bitcast(I32), x_rows[:, :X_FIRST])
-        load_scale_rows(scale_table[:], x_scales[0])
-        nc.sync.dma_start(x_table[:, X_FIRST:].bitcast(I32), x_rows[:, X_FIRST:])
-
         w1_codes = keep.tile([P, 2 * N], U8, name="w1_codes", align_bytes=64)
         nc.sync.dma_start(w1_codes[:].bitcast(I32), w1_words[0].bitcast(I32))
+        w1_scale = keep.tile([P, N], U8, name="w1_scale", align_bytes=64)
+        nc.vector.memset(w1_scale[:].bitcast(I32), 0)
         load_scale_rows(w1_scale[:], w1_scales[0])
+        nc.sync.dma_start(x_table[:, X_FIRST:].bitcast(I32), x_rows[:, X_FIRST:])
+        nc.vector.memset(scale_table[: P - 16, :].bitcast(I32), 0)
+        x_scale = keep.tile([P, S], U8, name="x_scale", align_bytes=64)
+        nc.vector.memset(x_scale[:].bitcast(I32), 0)
 
         w2_rows = w2.rearrange("(p j) c -> p j c", j=PACK)
         w2_raw = []
 
-        def load_w2_half(half, tag):
-            raw = keep.tile([P, PACK, HALF], F32, name="w2_raw%d" % half, tag=tag, align_bytes=64)
+        def load_w2_half(half, raw):
             nc.sync.dma_start(raw[:], w2_rows[:, :, half * HALF : (half + 1) * HALF])
             w2_raw.append(raw)
 
-        load_w2_half(0, "w2_first")
-        load_w2_half(1, "w2_second")
+        load_w2_half(0, keep.tile([P, PACK, HALF], F32, name="w2_raw0", align_bytes=64))
+        scale_picked = keep.tile([P, S], U8, name="scale_picked", align_bytes=64)
+        nc.vector.tensor_copy(scale_picked[:], scale_table[:].indirect(offsets[:]))
+        load_scale_rows(x_scale[:], scale_picked[P - 16 :, :])
+        load_w2_half(1, reused.tile([P, PACK, HALF], F32, name="w2_raw1", align_bytes=64, offset=1024))
 
-        x_scale = keep.tile([P, S], U8, name="x_scale", align_bytes=64)
-        nc.vector.tensor_copy(x_scale[:], scale_table[:].indirect(offsets[:]))
-
-        w3_tile = keep.tile([P, 3 * N], U8, name="w3_tile", tag="table", align_bytes=64)
+        w3_tile = reused.tile([P, 3 * N], U8, name="w3_tile", align_bytes=64, offset=0)
         w3_codes = w3_tile[:, : 2 * N]
         w3_scale = w3_tile[:, 2 * N :]
-        nc.sync.dma_start(w3_codes.bitcast(I32), w3_words[0].bitcast(I32))
         nc.vector.memset(w3_scale.bitcast(I32), 0)
+        nc.sync.dma_start(w3_codes.bitcast(I32), w3_words[0].bitcast(I32))
         load_scale_rows(w3_scale, w3_scales[0])
 
         x_codes = []
@@ -188,7 +189,8 @@ def tile_picked_lora_relu_p_kernel(
                             nc.vector.tensor_copy(staged[:], bank[:])
                         else:
                             nc.scalar.copy(staged[:], bank[:])
-                        nc.sync.dma_start(
+                        queue = nc.scalar if piece == len(PIECES) - 2 else nc.sync
+                        queue.dma_start(
                             out_view[:, m_tiles[0] : m_tiles[-1] + 1, first * CHUNK : (first + PAIR) * CHUNK], staged[:]
                         )
 

@@ -156,7 +156,7 @@ def tile_picked_lora_relu_p_kernel(
                     start=True,
                     stop=True,
                 )
-            h = keep.tile([P, CHUNK, PACK], BF16, name="h%d" % c, align_bytes=64)
+            h = keep.tile([P, CHUNK, PACK], BF16, name="h%d" % (0 if c == 3 else c), align_bytes=64)
             src = bank[:].rearrange("p t n -> p n t")
             if c % 2 == 0:
                 nc.scalar.activation(h[:], src, RELU)
@@ -184,15 +184,14 @@ def tile_picked_lora_relu_p_kernel(
                     bank = out_banks[piece]
                     out_pass(bank, c - first, m_tiles, w3_codes, w3_scale, h_codes[:].bitcast(FP8X4), h_scale[:], False, last)
                     if last:
-                        staged = keep.tile([P, len(m_tiles), PAIR * CHUNK], F32, name="staged%d" % piece)
-                        if piece == len(PIECES) - 1:
-                            nc.vector.tensor_copy(staged[:], bank[:])
-                        else:
-                            nc.scalar.copy(staged[:], bank[:])
-                        queue = nc.scalar if piece == len(PIECES) - 2 else nc.sync
-                        queue.dma_start(
-                            out_view[:, m_tiles[0] : m_tiles[-1] + 1, first * CHUNK : (first + PAIR) * CHUNK], staged[:]
-                        )
+                        for place, mt in enumerate(m_tiles):
+                            staged = keep.tile([P, PAIR * CHUNK], F32, name="staged%d_%d" % (piece, mt))
+                            if piece == len(PIECES) - 1:
+                                nc.vector.tensor_copy(staged[:], bank[:, place, :])
+                            else:
+                                nc.scalar.copy(staged[:], bank[:, place, :])
+                            queue = nc.scalar if piece == len(PIECES) - 2 else nc.sync
+                            queue.dma_start(out_view[:, mt, first * CHUNK : (first + PAIR) * CHUNK], staged[:])
 
         for step in range(CHUNKS + LAG):
             if step < CHUNKS:

@@ -50,7 +50,7 @@ def tile_picked_lora_relu_p_kernel(
                 nc.sync.dma_start(plane[r:P:32, :].bitcast(I32), rows[r:16:4, :].bitcast(I32))
 
         scale_table = reused.tile([P, T], U8, name="scale_table", align_bytes=64, offset=0)
-        nc.sync.dma_start(scale_table[P - 16 :, :].bitcast(I32), x_scales[0].bitcast(I32))
+        nc.scalar.dma_start(scale_table[P - 16 :, :].bitcast(I32), x_scales[0].bitcast(I32))
         x_table = keep.tile([P, T], U32, name="x_table", align_bytes=64)
         x_rows = x_words[0].rearrange("p c r -> p (c r)").bitcast(I32)
         nc.sync.dma_start(x_table[:, :X_FIRST].bitcast(I32), x_rows[:, :X_FIRST])
@@ -143,25 +143,33 @@ def tile_picked_lora_relu_p_kernel(
 
         hidden = {}
 
-        def first_product(c):
-            bank = h_psum.tile([P, PACK, CHUNK], F32, name="h_bank")
+        def hidden_part(c, h, tokens, on_scalar):
+            width = tokens.stop - tokens.start
+            bank = h_psum.tile([P, PACK, width], F32, name="h_bank")
             rhs, rhs_scale = x_operand(c)
             for t in range(PACK):
                 nc.tensor.matmul_mx(
                     out=bank[:, t, :],
                     lhsT=w2_codes[:, t * P : (t + 1) * P].bitcast(FP8X4),
                     lhsT_scale=w2_scale[:, t * P : (t + 1) * P],
-                    rhs=rhs,
-                    rhs_scale=rhs_scale,
+                    rhs=rhs[:, tokens],
+                    rhs_scale=rhs_scale[:, tokens],
                     start=True,
                     stop=True,
                 )
-            h = keep.tile([P, CHUNK, PACK], BF16, name="h%d" % (0 if c == 3 else c), align_bytes=64)
             src = bank[:].rearrange("p t n -> p n t")
-            if c % 2 == 0:
-                nc.scalar.activation(h[:], src, RELU)
+            if on_scalar:
+                nc.scalar.activation(h[:, tokens, :], src, RELU)
             else:
-                nc.vector.tensor_scalar_max(h[:], src, 0.0)
+                nc.vector.tensor_scalar_max(h[:, tokens, :], src, 0.0)
+
+        def first_product(c):
+            h = keep.tile([P, CHUNK, PACK], BF16, name="h%d" % (0 if c == 3 else c), align_bytes=64)
+            if c == CHUNKS - 1:
+                hidden_part(c, h, slice(0, CHUNK // 2), False)
+                hidden_part(c, h, slice(CHUNK // 2, CHUNK), True)
+            else:
+                hidden_part(c, h, slice(0, CHUNK), c % 2 == 0)
             hidden[c] = h
 
         out_view = out.rearrange("(mt p) s -> p mt s", p=P)

@@ -116,6 +116,17 @@ def tile_picked_lora_relu_p_kernel(
                 out_pass(bank, slot, m_tiles, w1_codes, w1_scale, rhs, rhs_scale, slot == 0, False)
             out_banks.append(bank)
 
+        for turn in range(2):
+            unread = h_psum.tile([P, N], F32, name="h_bank")
+            nc.tensor.matmul_mx(
+                out=unread[:],
+                lhsT=w1_codes[:, : 2 * P].bitcast(FP4X4),
+                lhsT_scale=w1_scale[:, :P],
+                rhs=x_codes[0][:, :N].bitcast(FP8X4),
+                rhs_scale=w1_scale[:],
+                start=True,
+                stop=True,
+            )
         for piece, (first, m_tiles) in enumerate(PIECES[:EARLY]):
             open_piece(out_psum, "out_bank%d" % piece, first, m_tiles)
 

@@ -24,10 +24,9 @@ GATHER = 512
 M_TILES = N // P
 HALF = H // 2
 HALF_M = HALF // PACK
-LAG = 4
-EARLY = 4
+EARLY = 3
 X_FIRST = 2048
-VECTOR_M = 40
+VECTOR_M = 32
 PIECES = ((0, (0, 1)), (2, (0, 1)), (4, (0, 1)), (6, (0,)), (6, (1,)))
 PAIR = 2
 
@@ -40,7 +39,7 @@ def tile_picked_lora_relu_p_kernel(
         keep = ctx.enter_context(tc.tile_pool(name="keep", bufs=1))
         reused = ctx.enter_context(tc.tile_pool(name="reused", bufs=1))
         out_psum = ctx.enter_context(tc.psum_pool(name="out_psum", bufs=1))
-        h_psum = ctx.enter_context(tc.psum_pool(name="h_psum", bufs=4))
+        h_psum = ctx.enter_context(tc.psum_pool(name="h_psum", bufs=5))
 
         offsets = keep.tile([P, S // 16], U16, name="offsets")
         nc.sync.dma_start(offsets[:], offs)
@@ -54,12 +53,12 @@ def tile_picked_lora_relu_p_kernel(
         x_table = keep.tile([P, T], U32, name="x_table", align_bytes=64)
         x_rows = x_words[0].rearrange("p c r -> p (c r)").bitcast(I32)
         nc.sync.dma_start(x_table[:, :X_FIRST].bitcast(I32), x_rows[:, :X_FIRST])
-        w1_codes = keep.tile([P, 2 * N], U8, name="w1_codes", align_bytes=64)
-        nc.sync.dma_start(w1_codes[:].bitcast(I32), w1_words[0].bitcast(I32))
         w1_scale = keep.tile([P, N], U8, name="w1_scale", align_bytes=64)
         nc.vector.memset(w1_scale[:].bitcast(I32), 0)
         load_scale_rows(w1_scale[:], w1_scales[0])
         nc.sync.dma_start(x_table[:, X_FIRST:].bitcast(I32), x_rows[:, X_FIRST:])
+        w1_codes = keep.tile([P, 2 * N], U8, name="w1_codes", align_bytes=64)
+        nc.sync.dma_start(w1_codes[:].bitcast(I32), w1_words[0].bitcast(I32))
         nc.vector.memset(scale_table[: P - 16, :].bitcast(I32), 0)
         x_scale = keep.tile([P, S], U8, name="x_scale", align_bytes=64)
         nc.vector.memset(x_scale[:].bitcast(I32), 0)
@@ -116,7 +115,7 @@ def tile_picked_lora_relu_p_kernel(
                 out_pass(bank, slot, m_tiles, w1_codes, w1_scale, rhs, rhs_scale, slot == 0, False)
             out_banks.append(bank)
 
-        for turn in range(2):
+        for turn in range(1):
             unread = h_psum.tile([P, N], F32, name="h_bank")
             nc.tensor.matmul_mx(
                 out=unread[:],
@@ -140,7 +139,8 @@ def tile_picked_lora_relu_p_kernel(
             if half == 0:
                 nc.scalar.activation(dst, src, COPY)
             else:
-                nc.vector.tensor_copy(dst[:, :VECTOR_M], src[:, :VECTOR_M])
+                for t in range(0, PACK, 2):
+                    nc.vector.tensor_copy(dst[:, :VECTOR_M, :, t : t + 2], src[:, :VECTOR_M, :, t : t + 2])
                 nc.scalar.activation(dst[:, VECTOR_M:], src[:, VECTOR_M:], COPY)
             grouped.append(tile)
         for half in range(2):
@@ -154,34 +154,50 @@ def tile_picked_lora_relu_p_kernel(
 
         hidden = {}
 
-        def hidden_part(c, h, tokens, on_scalar):
-            width = tokens.stop - tokens.start
-            bank = h_psum.tile([P, PACK, width], F32, name="h_bank")
+        def hidden_pass(bank, c, tokens, t):
             rhs, rhs_scale = x_operand(c)
-            for t in range(PACK):
-                nc.tensor.matmul_mx(
-                    out=bank[:, t, :],
-                    lhsT=w2_codes[:, t * P : (t + 1) * P].bitcast(FP8X4),
-                    lhsT_scale=w2_scale[:, t * P : (t + 1) * P],
-                    rhs=rhs[:, tokens],
-                    rhs_scale=rhs_scale[:, tokens],
-                    start=True,
-                    stop=True,
-                )
+            nc.tensor.matmul_mx(
+                out=bank[:, t, :],
+                lhsT=w2_codes[:, t * P : (t + 1) * P].bitcast(FP8X4),
+                lhsT_scale=w2_scale[:, t * P : (t + 1) * P],
+                rhs=rhs[:, tokens],
+                rhs_scale=rhs_scale[:, tokens],
+                start=True,
+                stop=True,
+            )
+
+        def leave_bank(bank, h, tokens, on_scalar):
             src = bank[:].rearrange("p t n -> p n t")
             if on_scalar:
                 nc.scalar.activation(h[:, tokens, :], src, RELU)
             else:
                 nc.vector.tensor_scalar_max(h[:, tokens, :], src, 0.0)
 
+        def hidden_part(c, h, tokens, on_scalar):
+            bank = h_psum.tile([P, PACK, tokens.stop - tokens.start], F32, name="h_bank")
+            for t in reversed(range(PACK)):
+                hidden_pass(bank, c, tokens, t)
+            leave_bank(bank, h, tokens, on_scalar)
+
+        def hidden_tile(c):
+            hidden[c] = keep.tile([P, CHUNK, PACK], BF16, name="h%d" % (0 if c == 3 else c), align_bytes=64)
+            return hidden[c]
+
+        def first_pair():
+            banks = [h_psum.tile([P, PACK, CHUNK], F32, name="h_bank") for c in range(PAIR)]
+            for t in range(PACK):
+                for c in range(PAIR):
+                    hidden_pass(banks[c], c, slice(0, CHUNK), t)
+            for c in range(PAIR):
+                leave_bank(banks[c], hidden_tile(c), slice(0, CHUNK), c % 2 == 0)
+
         def first_product(c):
-            h = keep.tile([P, CHUNK, PACK], BF16, name="h%d" % (0 if c == 3 else c), align_bytes=64)
+            h = hidden_tile(c)
             if c == CHUNKS - 1:
                 hidden_part(c, h, slice(0, CHUNK // 2), False)
                 hidden_part(c, h, slice(CHUNK // 2, CHUNK), True)
             else:
                 hidden_part(c, h, slice(0, CHUNK), c % 2 == 0)
-            hidden[c] = h
 
         out_view = out.rearrange("(mt p) s -> p mt s", p=P)
 
@@ -212,15 +228,19 @@ def tile_picked_lora_relu_p_kernel(
                             queue = nc.scalar if piece == len(PIECES) - 2 else nc.sync
                             queue.dma_start(out_view[:, mt, first * CHUNK : (first + PAIR) * CHUNK], staged[:])
 
-        for step in range(CHUNKS + LAG):
-            if step < CHUNKS:
-                first_product(step)
-                if step % 2 == 1:
-                    quantise_hidden(step - 1)
-                    quantise_hidden(step)
-            if step == CHUNKS:
-                for first, m_tiles in PIECES[EARLY:]:
-                    open_piece(h_psum, "h_bank", first, m_tiles)
-            if step >= LAG and step % 2 == 0:
-                second_product(step - LAG)
-                second_product(step - LAG + 1)
+        first_pair()
+        for c in range(1, CHUNKS):
+            if c == CHUNKS - 1:
+                second_product(0)
+                second_product(1)
+            if c >= PAIR:
+                first_product(c)
+            if c % 2 == 1:
+                quantise_hidden(c - 1)
+                quantise_hidden(c)
+        second_product(2)
+        second_product(3)
+        for first, m_tiles in PIECES[EARLY:]:
+            open_piece(h_psum, "h_bank", first, m_tiles)
+        for c in range(4, CHUNKS):
+            second_product(c)

@@ -26,9 +26,11 @@ HALF = H // 2
 HALF_M = HALF // PACK
 EARLY = 3
 X_FIRST = 2048
-VECTOR_M = 32
+VECTOR_M = 40
 PIECES = ((0, (0, 1)), (2, (0, 1)), (4, (0, 1)), (6, (0,)), (6, (1,)))
 PAIR = 2
+WARM_UPS = 4
+TWO_ONES = 0x3F803F80
 
 
 def tile_picked_lora_relu_p_kernel(
@@ -74,7 +76,7 @@ def tile_picked_lora_relu_p_kernel(
         scale_picked = keep.tile([P, S], U8, name="scale_picked", align_bytes=64)
         nc.vector.tensor_copy(scale_picked[:], scale_table[:].indirect(offsets[:]))
         load_scale_rows(x_scale[:], scale_picked[P - 16 :, :])
-        load_w2_half(1, reused.tile([P, PACK, HALF], F32, name="w2_raw1", align_bytes=64, offset=1024))
+        load_w2_half(1, reused.tile([P, PACK, HALF], F32, name="w2_raw1", align_bytes=64, offset=3072))
 
         w3_tile = reused.tile([P, 3 * N], U8, name="w3_tile", align_bytes=64, offset=0)
         w3_codes = w3_tile[:, : 2 * N]
@@ -82,6 +84,12 @@ def tile_picked_lora_relu_p_kernel(
         nc.vector.memset(w3_scale.bitcast(I32), 0)
         nc.sync.dma_start(w3_codes.bitcast(I32), w3_words[0].bitcast(I32))
         load_scale_rows(w3_scale, w3_scales[0])
+
+        ones = reused.tile([P, PACK * N], BF16, name="ones", align_bytes=64, offset=1024)
+        nc.vector.memset(ones[:].bitcast(I32), TWO_ONES)
+        ones_codes = keep.tile([P, N], U32, name="ones_codes", align_bytes=64)
+        ones_scale = keep.tile([P, N], U8, name="ones_scale", align_bytes=64)
+        nc.vector.quantize_mx(out=ones_codes[:].bitcast(FP8X4), scales=ones_scale[:], in_=ones[:])
 
         x_codes = []
         for g in range(S // GATHER):
@@ -115,14 +123,14 @@ def tile_picked_lora_relu_p_kernel(
                 out_pass(bank, slot, m_tiles, w1_codes, w1_scale, rhs, rhs_scale, slot == 0, False)
             out_banks.append(bank)
 
-        for turn in range(1):
+        for turn in range(WARM_UPS):
             unread = h_psum.tile([P, N], F32, name="h_bank")
             nc.tensor.matmul_mx(
                 out=unread[:],
                 lhsT=w1_codes[:, : 2 * P].bitcast(FP4X4),
                 lhsT_scale=w1_scale[:, :P],
-                rhs=x_codes[0][:, :N].bitcast(FP8X4),
-                rhs_scale=w1_scale[:],
+                rhs=ones_codes[:].bitcast(FP8X4),
+                rhs_scale=ones_scale[:],
                 start=True,
                 stop=True,
             )
@@ -131,26 +139,23 @@ def tile_picked_lora_relu_p_kernel(
 
         w2_codes = keep.tile([P, H], U32, name="w2_codes", align_bytes=64)
         w2_scale = keep.tile([P, H], U8, name="w2_scale", align_bytes=64)
-        grouped = []
+        grouped = keep.tile([P, PACK, P, PACK], BF16, name="w2_grouped", align_bytes=64)
         for half in range(2):
-            tile = keep.tile([P, PACK, HALF_M, PACK], BF16, name="w2_grouped%d" % half, align_bytes=64)
             src = w2_raw[half][:].rearrange("p j (m t) -> p m j t", t=PACK)
-            dst = tile[:].rearrange("p t m j -> p m j t")
+            dst = grouped[:, :, half * HALF_M : (half + 1) * HALF_M, :].rearrange("p t m j -> p m j t")
             if half == 0:
                 nc.scalar.activation(dst, src, COPY)
             else:
                 for t in range(0, PACK, 2):
                     nc.vector.tensor_copy(dst[:, :VECTOR_M, :, t : t + 2], src[:, :VECTOR_M, :, t : t + 2])
                 nc.scalar.activation(dst[:, VECTOR_M:], src[:, VECTOR_M:], COPY)
-            grouped.append(tile)
-        for half in range(2):
-            for t in range(PACK):
-                cols = slice(t * P + half * HALF_M, t * P + (half + 1) * HALF_M)
-                nc.vector.quantize_mx(
-                    out=w2_codes[:, cols].bitcast(FP8X4),
-                    scales=w2_scale[:, cols],
-                    in_=grouped[half][:, t, :, :].rearrange("p m j -> p (m j)"),
-                )
+        for t in range(PACK):
+            cols = slice(t * P, (t + 1) * P)
+            nc.vector.quantize_mx(
+                out=w2_codes[:, cols].bitcast(FP8X4),
+                scales=w2_scale[:, cols],
+                in_=grouped[:, t, :, :].rearrange("p m j -> p (m j)"),
+            )
 
         hidden = {}
 

@@ -29,7 +29,7 @@ X_FIRST = 2048
 VECTOR_M = 40
 PIECES = ((0, (0, 1)), (2, (0, 1)), (4, (0, 1)), (6, (0,)), (6, (1,)))
 PAIR = 2
-WARM_UPS = 4
+WARM_UPS = 6
 TWO_ONES = 0x3F803F80
 
 
@@ -127,8 +127,8 @@ def tile_picked_lora_relu_p_kernel(
             unread = h_psum.tile([P, N], F32, name="h_bank")
             nc.tensor.matmul_mx(
                 out=unread[:],
-                lhsT=w1_codes[:, : 2 * P].bitcast(FP4X4),
-                lhsT_scale=w1_scale[:, :P],
+                lhsT=ones_codes[:, :P].bitcast(FP8X4),
+                lhsT_scale=ones_scale[:, :P],
                 rhs=ones_codes[:].bitcast(FP8X4),
                 rhs_scale=ones_scale[:],
                 start=True,

@@ -29,8 +29,6 @@ X_FIRST = 2048
 VECTOR_M = 40
 PIECES = ((0, (0, 1)), (2, (0, 1)), (4, (0, 1)), (6, (0,)), (6, (1,)))
 PAIR = 2
-WARM_UPS = 6
-TWO_ONES = 0x3F803F80
 
 
 def tile_picked_lora_relu_p_kernel(
@@ -85,12 +83,6 @@ def tile_picked_lora_relu_p_kernel(
         nc.sync.dma_start(w3_codes.bitcast(I32), w3_words[0].bitcast(I32))
         load_scale_rows(w3_scale, w3_scales[0])
 
-        ones = reused.tile([P, PACK * N], BF16, name="ones", align_bytes=64, offset=1024)
-        nc.vector.memset(ones[:].bitcast(I32), TWO_ONES)
-        ones_codes = keep.tile([P, N], U32, name="ones_codes", align_bytes=64)
-        ones_scale = keep.tile([P, N], U8, name="ones_scale", align_bytes=64)
-        nc.vector.quantize_mx(out=ones_codes[:].bitcast(FP8X4), scales=ones_scale[:], in_=ones[:])
-
         x_codes = []
         for g in range(S // GATHER):
             picked = keep.tile([P, GATHER], U32, name="x_codes%d" % g, align_bytes=64)
@@ -123,17 +115,6 @@ def tile_picked_lora_relu_p_kernel(
                 out_pass(bank, slot, m_tiles, w1_codes, w1_scale, rhs, rhs_scale, slot == 0, False)
             out_banks.append(bank)
 
-        for turn in range(WARM_UPS):
-            unread = h_psum.tile([P, N], F32, name="h_bank")
-            nc.tensor.matmul_mx(
-                out=unread[:],
-                lhsT=ones_codes[:, :P].bitcast(FP8X4),
-                lhsT_scale=ones_scale[:, :P],
-                rhs=ones_codes[:].bitcast(FP8X4),
-                rhs_scale=ones_scale[:],
-                start=True,
-                stop=True,
-            )
         for piece, (first, m_tiles) in enumerate(PIECES[:EARLY]):
             open_piece(out_psum, "out_bank%d" % piece, first, m_tiles)
 

@@ -22,11 +22,10 @@ CHUNK = 128
 CHUNKS = S // CHUNK
 GATHER = 512
 M_TILES = N // P
-HALF = H // 2
-HALF_M = HALF // PACK
+ROWS = 2
 EARLY = 3
 X_FIRST = 2048
-VECTOR_M = 40
+VECTOR_M = (32, 80)
 PIECES = ((0, (0, 1)), (2, (0, 1)), (4, (0, 1)), (6, (0,)), (6, (1,)))
 PAIR = 2
 
@@ -67,14 +66,14 @@ def tile_picked_lora_relu_p_kernel(
         w2_raw = []
 
         def load_w2_half(half, raw):
-            nc.sync.dma_start(raw[:], w2_rows[:, :, half * HALF : (half + 1) * HALF])
+            nc.sync.dma_start(raw[:], w2_rows[:, half * ROWS : (half + 1) * ROWS, :])
             w2_raw.append(raw)
 
-        load_w2_half(0, keep.tile([P, PACK, HALF], F32, name="w2_raw0", align_bytes=64))
+        load_w2_half(0, keep.tile([P, ROWS, H], F32, name="w2_raw0", align_bytes=64))
         scale_picked = keep.tile([P, S], U8, name="scale_picked", align_bytes=64)
         nc.vector.tensor_copy(scale_picked[:], scale_table[:].indirect(offsets[:]))
         load_scale_rows(x_scale[:], scale_picked[P - 16 :, :])
-        load_w2_half(1, reused.tile([P, PACK, HALF], F32, name="w2_raw1", align_bytes=64, offset=3072))
+        load_w2_half(1, reused.tile([P, ROWS, H], F32, name="w2_raw1", align_bytes=64, offset=3072))
 
         w3_tile = reused.tile([P, 3 * N], U8, name="w3_tile", align_bytes=64, offset=0)
         w3_codes = w3_tile[:, : 2 * N]
@@ -123,13 +122,15 @@ def tile_picked_lora_relu_p_kernel(
         grouped = keep.tile([P, PACK, P, PACK], BF16, name="w2_grouped", align_bytes=64)
         for half in range(2):
             src = w2_raw[half][:].rearrange("p j (m t) -> p m j t", t=PACK)
-            dst = grouped[:, :, half * HALF_M : (half + 1) * HALF_M, :].rearrange("p t m j -> p m j t")
+            dst = grouped[:, :, :, half * ROWS : (half + 1) * ROWS].rearrange("p t m j -> p m j t")
+            share = VECTOR_M[half]
             if half == 0:
-                nc.scalar.activation(dst, src, COPY)
+                nc.scalar.activation(dst[:, share:], src[:, share:], COPY)
+                nc.vector.tensor_copy(dst[:, :share], src[:, :share])
             else:
                 for t in range(0, PACK, 2):
-                    nc.vector.tensor_copy(dst[:, :VECTOR_M, :, t : t + 2], src[:, :VECTOR_M, :, t : t + 2])
-                nc.scalar.activation(dst[:, VECTOR_M:], src[:, VECTOR_M:], COPY)
+                    nc.vector.tensor_copy(dst[:, :share, :, t : t + 2], src[:, :share, :, t : t + 2])
+                    nc.scalar.activation(dst[:, share:, :, t : t + 2], src[:, share:, :, t : t + 2], COPY)
         for t in range(PACK):
             cols = slice(t * P, (t + 1) * P)
             nc.vector.quantize_mx(

@@ -26,7 +26,7 @@ ROWS = 2
 EARLY = 3
 X_FIRST = 2048
 VECTOR_M = (32, 80)
-PIECES = ((0, (0, 1)), (2, (0, 1)), (4, (0, 1)), (6, (0,)), (6, (1,)))
+PIECES = ((0, (0, 1)), (2, (0, 1)), (4, (0, 1)), (6, (0,)))
 PAIR = 2
 
 
@@ -208,11 +208,8 @@ def tile_picked_lora_relu_p_kernel(
                     if last:
                         for place, mt in enumerate(m_tiles):
                             staged = keep.tile([P, PAIR * CHUNK], F32, name="staged%d_%d" % (piece, mt))
-                            if piece == len(PIECES) - 1:
-                                nc.vector.tensor_copy(staged[:], bank[:, place, :])
-                            else:
-                                nc.scalar.copy(staged[:], bank[:, place, :])
-                            queue = nc.scalar if piece == len(PIECES) - 2 else nc.sync
+                            nc.scalar.copy(staged[:], bank[:, place, :])
+                            queue = nc.scalar if piece == len(PIECES) - 1 else nc.sync
                             queue.dma_start(out_view[:, mt, first * CHUNK : (first + PAIR) * CHUNK], staged[:])
 
         first_pair()
@@ -227,7 +224,19 @@ def tile_picked_lora_relu_p_kernel(
                 quantise_hidden(c)
         second_product(2)
         second_product(3)
-        for first, m_tiles in PIECES[EARLY:]:
-            open_piece(h_psum, "h_bank", first, m_tiles)
+        open_piece(h_psum, "h_bank", *PIECES[EARLY])
+        tail_banks = []
+        for c in range(CHUNKS - PAIR, CHUNKS):
+            bank = h_psum.tile([P, 1, CHUNK], F32, name="h_bank")
+            rhs, rhs_scale = x_operand(c)
+            out_pass(bank, 0, (1,), w1_codes, w1_scale, rhs, rhs_scale, True, False)
+            tail_banks.append(bank)
+        tail = keep.tile([P, PAIR * CHUNK], F32, name="tail")
         for c in range(4, CHUNKS):
+            if c >= CHUNKS - PAIR:
+                slot = c - CHUNKS + PAIR
+                h_codes, h_scale = quantised[c]
+                out_pass(tail_banks[slot], 0, (1,), w3_codes, w3_scale, h_codes[:].bitcast(FP8X4), h_scale[:], False, True)
+                nc.vector.tensor_copy(tail[:, slot * CHUNK : (slot + 1) * CHUNK], tail_banks[slot][:, 0, :])
             second_product(c)
+        nc.sync.dma_start(out_view[:, 1, (CHUNKS - PAIR) * CHUNK :], tail[:])

@@ -18,16 +18,18 @@ COPY = mybir.ActivationFunctionType.Copy
 
 P = 128
 PACK = 4
+SCALE_ROWS = K // 32
 CHUNK = 128
 CHUNKS = S // CHUNK
-GATHER = 512
-M_TILES = N // P
-ROWS = 2
-EARLY = 3
-X_FIRST = 2048
-VECTOR_M = (32, 80)
-PIECES = ((0, (0, 1)), (2, (0, 1)), (4, (0, 1)), (6, (0,)))
 PAIR = 2
+LAST_PAIR = CHUNKS - PAIR
+GATHER = 512
+ROW_TILES = N // P
+HIDDEN_BANKS = 5
+W2_ROWS = 2
+VECTOR_GROUPS = (32, 80)
+W3_OFFSET = 0
+W2_LAST_OFFSET = 3072
 
 
 def tile_picked_lora_relu_p_kernel(
@@ -38,44 +40,41 @@ def tile_picked_lora_relu_p_kernel(
         keep = ctx.enter_context(tc.tile_pool(name="keep", bufs=1))
         reused = ctx.enter_context(tc.tile_pool(name="reused", bufs=1))
         out_psum = ctx.enter_context(tc.psum_pool(name="out_psum", bufs=1))
-        h_psum = ctx.enter_context(tc.psum_pool(name="h_psum", bufs=5))
+        h_psum = ctx.enter_context(tc.psum_pool(name="h_psum", bufs=HIDDEN_BANKS))
 
         offsets = keep.tile([P, S // 16], U16, name="offsets")
         nc.sync.dma_start(offsets[:], offs)
 
         def load_scale_rows(plane, rows):
             for r in range(4):
-                nc.sync.dma_start(plane[r:P:32, :].bitcast(I32), rows[r:16:4, :].bitcast(I32))
+                nc.sync.dma_start(plane[r:P:32, :].bitcast(I32), rows[r:SCALE_ROWS:4, :].bitcast(I32))
 
         scale_table = reused.tile([P, T], U8, name="scale_table", align_bytes=64, offset=0)
-        nc.scalar.dma_start(scale_table[P - 16 :, :].bitcast(I32), x_scales[0].bitcast(I32))
+        nc.scalar.dma_start(scale_table[P - SCALE_ROWS :, :].bitcast(I32), x_scales[0].bitcast(I32))
+
         x_table = keep.tile([P, T], U32, name="x_table", align_bytes=64)
         x_rows = x_words[0].rearrange("p c r -> p (c r)").bitcast(I32)
-        nc.sync.dma_start(x_table[:, :X_FIRST].bitcast(I32), x_rows[:, :X_FIRST])
+        nc.sync.dma_start(x_table[:, : T // 2].bitcast(I32), x_rows[:, : T // 2])
         w1_scale = keep.tile([P, N], U8, name="w1_scale", align_bytes=64)
         nc.vector.memset(w1_scale[:].bitcast(I32), 0)
         load_scale_rows(w1_scale[:], w1_scales[0])
-        nc.sync.dma_start(x_table[:, X_FIRST:].bitcast(I32), x_rows[:, X_FIRST:])
+        nc.sync.dma_start(x_table[:, T // 2 :].bitcast(I32), x_rows[:, T // 2 :])
         w1_codes = keep.tile([P, 2 * N], U8, name="w1_codes", align_bytes=64)
         nc.sync.dma_start(w1_codes[:].bitcast(I32), w1_words[0].bitcast(I32))
-        nc.vector.memset(scale_table[: P - 16, :].bitcast(I32), 0)
+        nc.vector.memset(scale_table[: P - SCALE_ROWS, :].bitcast(I32), 0)
         x_scale = keep.tile([P, S], U8, name="x_scale", align_bytes=64)
         nc.vector.memset(x_scale[:].bitcast(I32), 0)
 
         w2_rows = w2.rearrange("(p j) c -> p j c", j=PACK)
-        w2_raw = []
-
-        def load_w2_half(half, raw):
-            nc.sync.dma_start(raw[:], w2_rows[:, half * ROWS : (half + 1) * ROWS, :])
-            w2_raw.append(raw)
-
-        load_w2_half(0, keep.tile([P, ROWS, H], F32, name="w2_raw0", align_bytes=64))
+        w2_first = keep.tile([P, W2_ROWS, H], F32, name="w2_first", align_bytes=64)
+        nc.sync.dma_start(w2_first[:], w2_rows[:, :W2_ROWS, :])
         scale_picked = keep.tile([P, S], U8, name="scale_picked", align_bytes=64)
         nc.vector.tensor_copy(scale_picked[:], scale_table[:].indirect(offsets[:]))
-        load_scale_rows(x_scale[:], scale_picked[P - 16 :, :])
-        load_w2_half(1, reused.tile([P, ROWS, H], F32, name="w2_raw1", align_bytes=64, offset=3072))
+        load_scale_rows(x_scale[:], scale_picked[P - SCALE_ROWS :, :])
+        w2_last = reused.tile([P, W2_ROWS, H], F32, name="w2_last", align_bytes=64, offset=W2_LAST_OFFSET)
+        nc.sync.dma_start(w2_last[:], w2_rows[:, W2_ROWS:, :])
 
-        w3_tile = reused.tile([P, 3 * N], U8, name="w3_tile", align_bytes=64, offset=0)
+        w3_tile = reused.tile([P, 3 * N], U8, name="w3_tile", align_bytes=64, offset=W3_OFFSET)
         w3_codes = w3_tile[:, : 2 * N]
         w3_scale = w3_tile[:, 2 * N :]
         nc.vector.memset(w3_scale.bitcast(I32), 0)
@@ -93,44 +92,47 @@ def tile_picked_lora_relu_p_kernel(
             g, first = divmod(c * CHUNK, GATHER)
             return x_codes[g][:, first : first + CHUNK].bitcast(FP8X4), x_scale[:, c * CHUNK : (c + 1) * CHUNK]
 
-        def out_pass(bank, slot, m_tiles, codes, plane, rhs, rhs_scale, start, stop):
-            for place, mt in enumerate(m_tiles):
-                nc.tensor.matmul_mx(
-                    out=bank[:, place, slot * CHUNK : (slot + 1) * CHUNK],
-                    lhsT=codes[:, 2 * P * mt : 2 * P * (mt + 1)].bitcast(FP4X4),
-                    lhsT_scale=plane[:, P * mt : P * (mt + 1)],
-                    rhs=rhs,
-                    rhs_scale=rhs_scale,
-                    start=start and place == 0,
-                    stop=stop and place == len(m_tiles) - 1,
-                )
+        def out_pass(target, row_tile, codes, plane, operand, start, stop):
+            nc.tensor.matmul_mx(
+                out=target,
+                lhsT=codes[:, 2 * P * row_tile : 2 * P * (row_tile + 1)].bitcast(FP4X4),
+                lhsT_scale=plane[:, P * row_tile : P * (row_tile + 1)],
+                rhs=operand[0],
+                rhs_scale=operand[1],
+                start=start,
+                stop=stop,
+            )
+
+        def pair_columns(c):
+            return slice(c % PAIR * CHUNK, (c % PAIR + 1) * CHUNK)
 
         out_banks = []
-
-        def open_piece(pool, name, first, m_tiles):
-            bank = pool.tile([P, len(m_tiles), PAIR * CHUNK], F32, name=name)
-            for slot in range(PAIR):
-                rhs, rhs_scale = x_operand(first + slot)
-                out_pass(bank, slot, m_tiles, w1_codes, w1_scale, rhs, rhs_scale, slot == 0, False)
+        for pair in range(LAST_PAIR // PAIR):
+            bank = out_psum.tile([P, ROW_TILES, PAIR * CHUNK], F32, name="out_bank%d" % pair)
+            for c in range(pair * PAIR, (pair + 1) * PAIR):
+                for row_tile in range(ROW_TILES):
+                    start = c % PAIR == 0 and row_tile == 0
+                    out_pass(bank[:, row_tile, pair_columns(c)], row_tile, w1_codes, w1_scale, x_operand(c), start, False)
             out_banks.append(bank)
-
-        for piece, (first, m_tiles) in enumerate(PIECES[:EARLY]):
-            open_piece(out_psum, "out_bank%d" % piece, first, m_tiles)
 
         w2_codes = keep.tile([P, H], U32, name="w2_codes", align_bytes=64)
         w2_scale = keep.tile([P, H], U8, name="w2_scale", align_bytes=64)
         grouped = keep.tile([P, PACK, P, PACK], BF16, name="w2_grouped", align_bytes=64)
-        for half in range(2):
-            src = w2_raw[half][:].rearrange("p j (m t) -> p m j t", t=PACK)
-            dst = grouped[:, :, :, half * ROWS : (half + 1) * ROWS].rearrange("p t m j -> p m j t")
-            share = VECTOR_M[half]
-            if half == 0:
-                nc.scalar.activation(dst[:, share:], src[:, share:], COPY)
-                nc.vector.tensor_copy(dst[:, :share], src[:, :share])
-            else:
-                for t in range(0, PACK, 2):
-                    nc.vector.tensor_copy(dst[:, :share, :, t : t + 2], src[:, :share, :, t : t + 2])
-                    nc.scalar.activation(dst[:, share:, :, t : t + 2], src[:, share:, :, t : t + 2], COPY)
+
+        def cast_views(raw, first_row):
+            src = raw[:].rearrange("p j (m t) -> p m j t", t=PACK)
+            dst = grouped[:, :, :, first_row : first_row + W2_ROWS].rearrange("p t m j -> p m j t")
+            return dst, src
+
+        dst, src = cast_views(w2_first, 0)
+        share = VECTOR_GROUPS[0]
+        nc.scalar.activation(dst[:, share:], src[:, share:], COPY)
+        nc.vector.tensor_copy(dst[:, :share], src[:, :share])
+        dst, src = cast_views(w2_last, W2_ROWS)
+        share = VECTOR_GROUPS[1]
+        for t in range(0, PACK, 2):
+            nc.vector.tensor_copy(dst[:, :share, :, t : t + 2], src[:, :share, :, t : t + 2])
+            nc.scalar.activation(dst[:, share:, :, t : t + 2], src[:, share:, :, t : t + 2], COPY)
         for t in range(PACK):
             cols = slice(t * P, (t + 1) * P)
             nc.vector.quantize_mx(
@@ -167,7 +169,7 @@ def tile_picked_lora_relu_p_kernel(
             leave_bank(bank, h, tokens, on_scalar)
 
         def hidden_tile(c):
-            hidden[c] = keep.tile([P, CHUNK, PACK], BF16, name="h%d" % (0 if c == 3 else c), align_bytes=64)
+            hidden[c] = keep.tile([P, CHUNK, PACK], BF16, name="h%d" % c, align_bytes=64)
             return hidden[c]
 
         def first_pair():
@@ -186,8 +188,6 @@ def tile_picked_lora_relu_p_kernel(
             else:
                 hidden_part(c, h, slice(0, CHUNK), c % 2 == 0)
 
-        out_view = out.rearrange("(mt p) s -> p mt s", p=P)
-
         quantised = {}
 
         def quantise_hidden(c):
@@ -196,47 +196,48 @@ def tile_picked_lora_relu_p_kernel(
             nc.vector.quantize_mx(
                 out=h_codes[:].bitcast(FP8X4), scales=h_scale[:], in_=hidden[c][:].rearrange("p n t -> p (n t)")
             )
-            quantised[c] = (h_codes, h_scale)
+            quantised[c] = (h_codes[:].bitcast(FP8X4), h_scale[:])
 
-        def second_product(c):
-            h_codes, h_scale = quantised[c]
-            for piece, (first, m_tiles) in enumerate(PIECES):
-                if first <= c < first + PAIR:
-                    last = c == first + PAIR - 1
-                    bank = out_banks[piece]
-                    out_pass(bank, c - first, m_tiles, w3_codes, w3_scale, h_codes[:].bitcast(FP8X4), h_scale[:], False, last)
-                    if last:
-                        for place, mt in enumerate(m_tiles):
-                            staged = keep.tile([P, PAIR * CHUNK], F32, name="staged%d_%d" % (piece, mt))
-                            nc.scalar.copy(staged[:], bank[:, place, :])
-                            queue = nc.scalar if piece == len(PIECES) - 1 else nc.sync
-                            queue.dma_start(out_view[:, mt, first * CHUNK : (first + PAIR) * CHUNK], staged[:])
+        out_view = out.rearrange("(r p) s -> p r s", p=P)
+
+        def second_product(pair):
+            bank = out_banks[pair]
+            for c in range(pair * PAIR, (pair + 1) * PAIR):
+                for row_tile in range(ROW_TILES):
+                    stop = c % PAIR == PAIR - 1 and row_tile == ROW_TILES - 1
+                    out_pass(bank[:, row_tile, pair_columns(c)], row_tile, w3_codes, w3_scale, quantised[c], False, stop)
+            columns = slice(pair * PAIR * CHUNK, (pair + 1) * PAIR * CHUNK)
+            for row_tile in range(ROW_TILES):
+                staged = keep.tile([P, PAIR * CHUNK], F32, name="staged%d_%d" % (pair, row_tile))
+                nc.scalar.copy(staged[:], bank[:, row_tile, :])
+                nc.sync.dma_start(out_view[:, row_tile, columns], staged[:])
 
         first_pair()
-        for c in range(1, CHUNKS):
+        done = 0
+        for c in range(PAIR, CHUNKS):
             if c == CHUNKS - 1:
                 second_product(0)
-                second_product(1)
-            if c >= PAIR:
-                first_product(c)
+            first_product(c)
             if c % 2 == 1:
-                quantise_hidden(c - 1)
-                quantise_hidden(c)
-        second_product(2)
-        second_product(3)
-        open_piece(h_psum, "h_bank", *PIECES[EARLY])
+                ready = CHUNKS if c == CHUNKS - 1 else c
+                for d in range(done, ready):
+                    quantise_hidden(d)
+                done = ready
+        second_product(1)
+
+        tails = [(c, row_tile) for c in range(LAST_PAIR, CHUNKS) for row_tile in reversed(range(ROW_TILES))]
         tail_banks = []
-        for c in range(CHUNKS - PAIR, CHUNKS):
-            bank = h_psum.tile([P, 1, CHUNK], F32, name="h_bank")
-            rhs, rhs_scale = x_operand(c)
-            out_pass(bank, 0, (1,), w1_codes, w1_scale, rhs, rhs_scale, True, False)
+        for c, row_tile in tails:
+            bank = h_psum.tile([P, CHUNK], F32, name="h_bank")
+            out_pass(bank[:], row_tile, w1_codes, w1_scale, x_operand(c), True, False)
             tail_banks.append(bank)
-        tail = keep.tile([P, PAIR * CHUNK], F32, name="tail")
-        for c in range(4, CHUNKS):
-            if c >= CHUNKS - PAIR:
-                slot = c - CHUNKS + PAIR
-                h_codes, h_scale = quantised[c]
-                out_pass(tail_banks[slot], 0, (1,), w3_codes, w3_scale, h_codes[:].bitcast(FP8X4), h_scale[:], False, True)
-                nc.vector.tensor_copy(tail[:, slot * CHUNK : (slot + 1) * CHUNK], tail_banks[slot][:, 0, :])
-            second_product(c)
-        nc.sync.dma_start(out_view[:, 1, (CHUNKS - PAIR) * CHUNK :], tail[:])
+        second_product(2)
+        tail = [keep.tile([P, PAIR * CHUNK], F32, name="tail%d" % row_tile) for row_tile in range(ROW_TILES)]
+        for bank, (c, row_tile) in zip(tail_banks, tails):
+            out_pass(bank[:], row_tile, w3_codes, w3_scale, quantised[c], False, True)
+            if row_tile == 0:
+                nc.scalar.copy(tail[row_tile][:, pair_columns(c)], bank[:])
+            else:
+                nc.vector.tensor_copy(tail[row_tile][:, pair_columns(c)], bank[:])
+        nc.scalar.dma_start(out_view[:, 0, LAST_PAIR * CHUNK :], tail[0][:])
+        nc.sync.dma_start(out_view[:, 1, LAST_PAIR * CHUNK :], tail[1][:])

@@ -28,8 +28,7 @@ ROW_TILES = N // P
 HIDDEN_BANKS = 5
 W2_ROWS = 2
 VECTOR_GROUPS = (32, 80)
-W3_OFFSET = 0
-W2_LAST_OFFSET = 3072
+LATE = PAIR * CHUNK
 
 
 def tile_picked_lora_relu_p_kernel(
@@ -38,7 +37,6 @@ def tile_picked_lora_relu_p_kernel(
     nc = tc.nc
     with ExitStack() as ctx:
         keep = ctx.enter_context(tc.tile_pool(name="keep", bufs=1))
-        reused = ctx.enter_context(tc.tile_pool(name="reused", bufs=1))
         out_psum = ctx.enter_context(tc.psum_pool(name="out_psum", bufs=1))
         h_psum = ctx.enter_context(tc.psum_pool(name="h_psum", bufs=HIDDEN_BANKS))
 
@@ -49,7 +47,7 @@ def tile_picked_lora_relu_p_kernel(
             for r in range(4):
                 nc.sync.dma_start(plane[r:P:32, :].bitcast(I32), rows[r:SCALE_ROWS:4, :].bitcast(I32))
 
-        scale_table = reused.tile([P, T], U8, name="scale_table", align_bytes=64, offset=0)
+        scale_table = keep.tile([P, T], U8, name="scale_table", align_bytes=64)
         nc.scalar.dma_start(scale_table[P - SCALE_ROWS :, :].bitcast(I32), x_scales[0].bitcast(I32))
 
         x_table = keep.tile([P, T], U32, name="x_table", align_bytes=64)
@@ -58,28 +56,32 @@ def tile_picked_lora_relu_p_kernel(
         w1_scale = keep.tile([P, N], U8, name="w1_scale", align_bytes=64)
         nc.vector.memset(w1_scale[:].bitcast(I32), 0)
         load_scale_rows(w1_scale[:], w1_scales[0])
+        staged = keep.tile([P, LATE + N], U8, name="staged_scales", align_bytes=64)
+        nc.sync.dma_start(staged[P - SCALE_ROWS :, LATE:].bitcast(I32), w3_scales[0].bitcast(I32))
         nc.sync.dma_start(x_table[:, T // 2 :].bitcast(I32), x_rows[:, T // 2 :])
         w1_codes = keep.tile([P, 2 * N], U8, name="w1_codes", align_bytes=64)
         nc.sync.dma_start(w1_codes[:].bitcast(I32), w1_words[0].bitcast(I32))
         nc.vector.memset(scale_table[: P - SCALE_ROWS, :].bitcast(I32), 0)
-        x_scale = keep.tile([P, S], U8, name="x_scale", align_bytes=64)
+        x_scale = keep.tile([P, S - LATE], U8, name="x_scale", align_bytes=64)
         nc.vector.memset(x_scale[:].bitcast(I32), 0)
+        late_planes = keep.tile([P, LATE + N], U8, name="late_planes", align_bytes=64)
+        nc.vector.memset(late_planes[:].bitcast(I32), 0)
 
         w2_rows = w2.rearrange("(p j) c -> p j c", j=PACK)
         w2_first = keep.tile([P, W2_ROWS, H], F32, name="w2_first", align_bytes=64)
         nc.sync.dma_start(w2_first[:], w2_rows[:, :W2_ROWS, :])
-        scale_picked = keep.tile([P, S], U8, name="scale_picked", align_bytes=64)
-        nc.vector.tensor_copy(scale_picked[:], scale_table[:].indirect(offsets[:]))
+        scale_picked = keep.tile([P, S - LATE], U8, name="scale_picked", align_bytes=64)
+        nc.vector.tensor_copy(scale_picked[:], scale_table[:].indirect(offsets[:, : (S - LATE) // 16]))
         load_scale_rows(x_scale[:], scale_picked[P - SCALE_ROWS :, :])
-        w2_last = reused.tile([P, W2_ROWS, H], F32, name="w2_last", align_bytes=64, offset=W2_LAST_OFFSET)
+        w2_last = keep.tile([P, W2_ROWS, H], F32, name="w2_last", align_bytes=64)
         nc.sync.dma_start(w2_last[:], w2_rows[:, W2_ROWS:, :])
-
-        w3_tile = reused.tile([P, 3 * N], U8, name="w3_tile", align_bytes=64, offset=W3_OFFSET)
-        w3_codes = w3_tile[:, : 2 * N]
-        w3_scale = w3_tile[:, 2 * N :]
-        nc.vector.memset(w3_scale.bitcast(I32), 0)
-        nc.sync.dma_start(w3_codes.bitcast(I32), w3_words[0].bitcast(I32))
-        load_scale_rows(w3_scale, w3_scales[0])
+        late_picked = keep.tile([P, T // 8], U8, name="late_picked", align_bytes=64)
+        nc.vector.tensor_copy(late_picked[:], scale_table[:].indirect(offsets[:, (S - T // 8) // 16 :]))
+        nc.vector.tensor_copy(staged[:, :LATE].bitcast(I32), late_picked[:, T // 8 - LATE :].bitcast(I32))
+        load_scale_rows(late_planes[:], staged[P - SCALE_ROWS :, :])
+        w3_codes = keep.tile([P, 2 * N], U8, name="w3_codes", align_bytes=64)
+        nc.sync.dma_start(w3_codes[:].bitcast(I32), w3_words[0].bitcast(I32))
+        w3_scale = late_planes[:, LATE:]
 
         x_codes = []
         for g in range(S // GATHER):
@@ -90,7 +92,8 @@ def tile_picked_lora_relu_p_kernel(
 
         def x_operand(c):
             g, first = divmod(c * CHUNK, GATHER)
-            return x_codes[g][:, first : first + CHUNK].bitcast(FP8X4), x_scale[:, c * CHUNK : (c + 1) * CHUNK]
+            plane, place = (x_scale, c) if c < LAST_PAIR else (late_planes, c - LAST_PAIR)
+            return x_codes[g][:, first : first + CHUNK].bitcast(FP8X4), plane[:, place * CHUNK : (place + 1) * CHUNK]
 
         def out_pass(target, row_tile, codes, plane, operand, start, stop):
             nc.tensor.matmul_mx(

@@ -19,16 +19,17 @@ COPY = mybir.ActivationFunctionType.Copy
 P = 128
 PACK = 4
 SCALE_ROWS = K // 32
+STAGE_FIRST = P - SCALE_ROWS
 CHUNK = 128
 CHUNKS = S // CHUNK
 PAIR = 2
-LAST_PAIR = CHUNKS - PAIR
+PAIRS = CHUNKS // PAIR
 GATHER = 512
 ROW_TILES = N // P
 HIDDEN_BANKS = 5
 W2_ROWS = 2
-VECTOR_GROUPS = (32, 80)
 LATE = PAIR * CHUNK
+VECTOR_GROUPS = (32, 80)
 
 
 def tile_picked_lora_relu_p_kernel(
@@ -83,6 +84,8 @@ def tile_picked_lora_relu_p_kernel(
         nc.sync.dma_start(w3_codes[:].bitcast(I32), w3_words[0].bitcast(I32))
         w3_scale = late_planes[:, LATE:]
 
+        w2_raw = [w2_first, w2_last]
+
         x_codes = []
         for g in range(S // GATHER):
             picked = keep.tile([P, GATHER], U32, name="x_codes%d" % g, align_bytes=64)
@@ -90,10 +93,10 @@ def tile_picked_lora_relu_p_kernel(
             nc.vector.tensor_copy(picked[:], x_table[:].indirect(offsets[:, g * columns : (g + 1) * columns]))
             x_codes.append(picked)
 
-        def x_operand(c):
-            g, first = divmod(c * CHUNK, GATHER)
-            plane, place = (x_scale, c) if c < LAST_PAIR else (late_planes, c - LAST_PAIR)
-            return x_codes[g][:, first : first + CHUNK].bitcast(FP8X4), plane[:, place * CHUNK : (place + 1) * CHUNK]
+        def x_operand(first, count):
+            g, at = divmod(first, GATHER)
+            plane, place = (x_scale, first) if first < S - LATE else (late_planes, first - (S - LATE))
+            return x_codes[g][:, at : at + count].bitcast(FP8X4), plane[:, place : place + count]
 
         def out_pass(target, row_tile, codes, plane, operand, start, stop):
             nc.tensor.matmul_mx(
@@ -109,29 +112,34 @@ def tile_picked_lora_relu_p_kernel(
         def pair_columns(c):
             return slice(c % PAIR * CHUNK, (c % PAIR + 1) * CHUNK)
 
-        out_banks = []
-        for pair in range(LAST_PAIR // PAIR):
-            bank = out_psum.tile([P, ROW_TILES, PAIR * CHUNK], F32, name="out_bank%d" % pair)
+        groups = {}
+
+        def open_bank(bank, pair, row_tiles):
             for c in range(pair * PAIR, (pair + 1) * PAIR):
-                for row_tile in range(ROW_TILES):
-                    start = c % PAIR == 0 and row_tile == 0
-                    out_pass(bank[:, row_tile, pair_columns(c)], row_tile, w1_codes, w1_scale, x_operand(c), start, False)
-            out_banks.append(bank)
+                for slot, row_tile in enumerate(row_tiles):
+                    start = c % PAIR == 0 and slot == 0
+                    operand = x_operand(c * CHUNK, CHUNK)
+                    out_pass(bank[:, slot, pair_columns(c)], row_tile, w1_codes, w1_scale, operand, start, False)
+                    groups[pair, row_tile] = (bank[:, slot, :], row_tile == row_tiles[-1])
+
+        for pair, row_tiles in ((0, [0, 1]), (1, [0, 1]), (2, [0, 1])):
+            bank = out_psum.tile([P, len(row_tiles), PAIR * CHUNK], F32, name="out_bank%d" % pair)
+            open_bank(bank, pair, row_tiles)
 
         w2_codes = keep.tile([P, H], U32, name="w2_codes", align_bytes=64)
         w2_scale = keep.tile([P, H], U8, name="w2_scale", align_bytes=64)
         grouped = keep.tile([P, PACK, P, PACK], BF16, name="w2_grouped", align_bytes=64)
 
-        def cast_views(raw, first_row):
-            src = raw[:].rearrange("p j (m t) -> p m j t", t=PACK)
-            dst = grouped[:, :, :, first_row : first_row + W2_ROWS].rearrange("p t m j -> p m j t")
+        def cast_views(part):
+            src = w2_raw[part][:].rearrange("p j (m t) -> p m j t", t=PACK)
+            dst = grouped[:, :, :, part * W2_ROWS : (part + 1) * W2_ROWS].rearrange("p t m j -> p m j t")
             return dst, src
 
-        dst, src = cast_views(w2_first, 0)
+        dst, src = cast_views(0)
         share = VECTOR_GROUPS[0]
         nc.scalar.activation(dst[:, share:], src[:, share:], COPY)
         nc.vector.tensor_copy(dst[:, :share], src[:, :share])
-        dst, src = cast_views(w2_last, W2_ROWS)
+        dst, src = cast_views(1)
         share = VECTOR_GROUPS[1]
         for t in range(0, PACK, 2):
             nc.vector.tensor_copy(dst[:, :share, :, t : t + 2], src[:, :share, :, t : t + 2])
@@ -146,54 +154,38 @@ def tile_picked_lora_relu_p_kernel(
 
         hidden = {}
 
-        def hidden_pass(bank, c, tokens, t):
-            rhs, rhs_scale = x_operand(c)
+        def hidden_tile(c, name):
+            hidden[c] = keep.tile([P, CHUNK, PACK], BF16, name=name, align_bytes=64)
+
+        def hidden_pass(bank, first, count, t):
+            rhs, rhs_scale = x_operand(first, count)
             nc.tensor.matmul_mx(
                 out=bank[:, t, :],
                 lhsT=w2_codes[:, t * P : (t + 1) * P].bitcast(FP8X4),
                 lhsT_scale=w2_scale[:, t * P : (t + 1) * P],
-                rhs=rhs[:, tokens],
-                rhs_scale=rhs_scale[:, tokens],
+                rhs=rhs,
+                rhs_scale=rhs_scale,
                 start=True,
                 stop=True,
             )
 
-        def leave_bank(bank, h, tokens, on_scalar):
+        def fill(first, count):
+            bank = h_psum.tile([P, PACK, count], F32, name="h_bank")
+            for t in reversed(range(PACK)):
+                hidden_pass(bank, first, count, t)
+            return bank
+
+        def empty(bank, first, count, on_scalar):
+            c, at = divmod(first, CHUNK)
             src = bank[:].rearrange("p t n -> p n t")
             if on_scalar:
-                nc.scalar.activation(h[:, tokens, :], src, RELU)
+                nc.scalar.activation(hidden[c][:, at : at + count, :], src, RELU)
             else:
-                nc.vector.tensor_scalar_max(h[:, tokens, :], src, 0.0)
-
-        def hidden_part(c, h, tokens, on_scalar):
-            bank = h_psum.tile([P, PACK, tokens.stop - tokens.start], F32, name="h_bank")
-            for t in reversed(range(PACK)):
-                hidden_pass(bank, c, tokens, t)
-            leave_bank(bank, h, tokens, on_scalar)
-
-        def hidden_tile(c):
-            hidden[c] = keep.tile([P, CHUNK, PACK], BF16, name="h%d" % c, align_bytes=64)
-            return hidden[c]
-
-        def first_pair():
-            banks = [h_psum.tile([P, PACK, CHUNK], F32, name="h_bank") for c in range(PAIR)]
-            for t in range(PACK):
-                for c in range(PAIR):
-                    hidden_pass(banks[c], c, slice(0, CHUNK), t)
-            for c in range(PAIR):
-                leave_bank(banks[c], hidden_tile(c), slice(0, CHUNK), c % 2 == 0)
-
-        def first_product(c):
-            h = hidden_tile(c)
-            if c == CHUNKS - 1:
-                hidden_part(c, h, slice(0, CHUNK // 2), False)
-                hidden_part(c, h, slice(CHUNK // 2, CHUNK), True)
-            else:
-                hidden_part(c, h, slice(0, CHUNK), c % 2 == 0)
+                nc.vector.tensor_scalar_max(hidden[c][:, at : at + count, :], src, 0.0)
 
         quantised = {}
 
-        def quantise_hidden(c):
+        def quantise(c):
             h_codes = keep.tile([P, CHUNK], U32, name="h_codes%d" % c, align_bytes=64)
             h_scale = keep.tile([P, CHUNK], U8, name="h_scale%d" % c, align_bytes=64)
             nc.vector.quantize_mx(
@@ -203,44 +195,74 @@ def tile_picked_lora_relu_p_kernel(
 
         out_view = out.rearrange("(r p) s -> p r s", p=P)
 
-        def second_product(pair):
-            bank = out_banks[pair]
-            for c in range(pair * PAIR, (pair + 1) * PAIR):
-                for row_tile in range(ROW_TILES):
-                    stop = c % PAIR == PAIR - 1 and row_tile == ROW_TILES - 1
-                    out_pass(bank[:, row_tile, pair_columns(c)], row_tile, w3_codes, w3_scale, quantised[c], False, stop)
-            columns = slice(pair * PAIR * CHUNK, (pair + 1) * PAIR * CHUNK)
+        def second_product(c):
             for row_tile in range(ROW_TILES):
-                staged = keep.tile([P, PAIR * CHUNK], F32, name="staged%d_%d" % (pair, row_tile))
-                nc.scalar.copy(staged[:], bank[:, row_tile, :])
-                nc.sync.dma_start(out_view[:, row_tile, columns], staged[:])
+                target, closes = groups[c // PAIR, row_tile]
+                stop = closes and c % PAIR == PAIR - 1
+                out_pass(target[:, pair_columns(c)], row_tile, w3_codes, w3_scale, quantised[c], False, stop)
 
-        first_pair()
-        done = 0
-        for c in range(PAIR, CHUNKS):
-            if c == CHUNKS - 1:
-                second_product(0)
-            first_product(c)
-            if c % 2 == 1:
-                ready = CHUNKS if c == CHUNKS - 1 else c
-                for d in range(done, ready):
-                    quantise_hidden(d)
-                done = ready
-        second_product(1)
-
-        tails = [(c, row_tile) for c in range(LAST_PAIR, CHUNKS) for row_tile in reversed(range(ROW_TILES))]
-        tail_banks = []
-        for c, row_tile in tails:
-            bank = h_psum.tile([P, CHUNK], F32, name="h_bank")
-            out_pass(bank[:], row_tile, w1_codes, w1_scale, x_operand(c), True, False)
-            tail_banks.append(bank)
-        second_product(2)
-        tail = [keep.tile([P, PAIR * CHUNK], F32, name="tail%d" % row_tile) for row_tile in range(ROW_TILES)]
-        for bank, (c, row_tile) in zip(tail_banks, tails):
-            out_pass(bank[:], row_tile, w3_codes, w3_scale, quantised[c], False, True)
-            if row_tile == 0:
-                nc.scalar.copy(tail[row_tile][:, pair_columns(c)], bank[:])
+        def leave(pair, row_tile, on_scalar, name):
+            columns = slice(pair * PAIR * CHUNK, (pair + 1) * PAIR * CHUNK)
+            staged = keep.tile([P, PAIR * CHUNK], F32, name=name, align_bytes=64)
+            if on_scalar:
+                nc.scalar.copy(staged[:], groups[pair, row_tile][0])
             else:
-                nc.vector.tensor_copy(tail[row_tile][:, pair_columns(c)], bank[:])
-        nc.scalar.dma_start(out_view[:, 0, LAST_PAIR * CHUNK :], tail[0][:])
-        nc.sync.dma_start(out_view[:, 1, LAST_PAIR * CHUNK :], tail[1][:])
+                nc.vector.tensor_copy(staged[:], groups[pair, row_tile][0])
+            nc.sync.dma_start(out_view[:, row_tile, columns], staged[:])
+
+        banks = [h_psum.tile([P, PACK, CHUNK], F32, name="h_bank") for c in range(PAIR)]
+        for t in range(PACK):
+            for c in range(PAIR):
+                hidden_pass(banks[c], c * CHUNK, CHUNK, t)
+        for c in range(PAIR):
+            hidden_tile(c, "h%d" % c)
+            empty(banks[c], c * CHUNK, CHUNK, c == 0)
+        def chunk(c, on_scalar):
+            hidden_tile(c, "h%d" % c)
+            empty(fill(c * CHUNK, CHUNK), c * CHUNK, CHUNK, on_scalar)
+
+        chunk(2, True)
+        chunk(3, False)
+        for c in range(0, 3):
+            quantise(c)
+        chunk(4, True)
+        chunk(5, False)
+        for c in range(3, 6):
+            quantise(c)
+        chunk(6, True)
+        second_product(0)
+        second_product(1)
+        leave(0, 0, True, "staged0_0")
+        leave(0, 1, True, "staged0_1")
+        half = CHUNK // 2
+        last = (CHUNKS - 1) * CHUNK
+        hidden_tile(7, "h7")
+        empty(fill(last, half), last, half, False)
+        empty(fill(last + half, half), last + half, half, True)
+        quantise(6)
+        quantise(7)
+        second_product(2)
+        second_product(3)
+        leave(1, 0, True, "staged1_0")
+        leave(1, 1, True, "staged1_1")
+        both = h_psum.tile([P, ROW_TILES, CHUNK], F32, name="h_bank")
+        for row_tile in range(ROW_TILES):
+            out_pass(both[:, row_tile, :], row_tile, w1_codes, w1_scale, x_operand(6 * CHUNK, CHUNK), row_tile == 0, False)
+        tail_banks = {}
+        for row_tile in reversed(range(ROW_TILES)):
+            tail_banks[row_tile] = h_psum.tile([P, CHUNK], F32, name="h_bank")
+            out_pass(tail_banks[row_tile][:], row_tile, w1_codes, w1_scale, x_operand(last, CHUNK), True, False)
+        second_product(4)
+        second_product(5)
+        leave(2, 0, False, "staged2_0")
+        leave(2, 1, False, "staged2_1")
+        tail = keep.tile([P, ROW_TILES, PAIR * CHUNK], F32, name="tail")
+        for row_tile in range(ROW_TILES):
+            out_pass(both[:, row_tile, :], row_tile, w3_codes, w3_scale, quantised[6], False, row_tile == 1)
+        nc.scalar.copy(tail[:, :, :CHUNK], both[:])
+        for row_tile in reversed(range(ROW_TILES)):
+            out_pass(tail_banks[row_tile][:], row_tile, w3_codes, w3_scale, quantised[7], False, True)
+        nc.vector.tensor_copy(tail[:, 1, CHUNK:], tail_banks[1][:])
+        nc.scalar.copy(tail[:, 0, CHUNK:], tail_banks[0][:])
+        nc.scalar.dma_start(out_view[:, 0, (CHUNKS - PAIR) * CHUNK :], tail[:, 0, :])
+        nc.sync.dma_start(out_view[:, 1, (CHUNKS - PAIR) * CHUNK :], tail[:, 1, :])

@@ -29,7 +29,7 @@ ROW_TILES = N // P
 HIDDEN_BANKS = 5
 W2_ROWS = 2
 LATE = PAIR * CHUNK
-VECTOR_GROUPS = (32, 80)
+VECTOR_GROUPS = (56, 88)
 
 
 def tile_picked_lora_relu_p_kernel(

@@ -29,7 +29,7 @@ ROW_TILES = N // P
 HIDDEN_BANKS = 5
 W2_ROWS = 2
 LATE = PAIR * CHUNK
-VECTOR_GROUPS = (56, 88)
+VECTOR_GROUPS = (48, 76)
 
 
 def tile_picked_lora_relu_p_kernel(

@@ -29,7 +29,7 @@ ROW_TILES = N // P
 HIDDEN_BANKS = 5
 W2_ROWS = 2
 LATE = PAIR * CHUNK
-VECTOR_GROUPS = (48, 76)
+VECTOR_GROUPS = (44, 82)
 
 
 def tile_picked_lora_relu_p_kernel(
@@ -60,8 +60,6 @@ def tile_picked_lora_relu_p_kernel(
         staged = keep.tile([P, LATE + N], U8, name="staged_scales", align_bytes=64)
         nc.sync.dma_start(staged[P - SCALE_ROWS :, LATE:].bitcast(I32), w3_scales[0].bitcast(I32))
         nc.sync.dma_start(x_table[:, T // 2 :].bitcast(I32), x_rows[:, T // 2 :])
-        w1_codes = keep.tile([P, 2 * N], U8, name="w1_codes", align_bytes=64)
-        nc.sync.dma_start(w1_codes[:].bitcast(I32), w1_words[0].bitcast(I32))
         nc.vector.memset(scale_table[: P - SCALE_ROWS, :].bitcast(I32), 0)
         x_scale = keep.tile([P, S - LATE], U8, name="x_scale", align_bytes=64)
         nc.vector.memset(x_scale[:].bitcast(I32), 0)
@@ -71,6 +69,8 @@ def tile_picked_lora_relu_p_kernel(
         w2_rows = w2.rearrange("(p j) c -> p j c", j=PACK)
         w2_first = keep.tile([P, W2_ROWS, H], F32, name="w2_first", align_bytes=64)
         nc.sync.dma_start(w2_first[:], w2_rows[:, :W2_ROWS, :])
+        w1_codes = keep.tile([P, 2 * N], U8, name="w1_codes", align_bytes=64)
+        nc.sync.dma_start(w1_codes[:].bitcast(I32), w1_words[0].bitcast(I32))
         scale_picked = keep.tile([P, S - LATE], U8, name="scale_picked", align_bytes=64)
         nc.vector.tensor_copy(scale_picked[:], scale_table[:].indirect(offsets[:, : (S - LATE) // 16]))
         load_scale_rows(x_scale[:], scale_picked[P - SCALE_ROWS :, :])

from contextlib import ExitStack

import concourse.mybir as mybir

K, T, S, H, N = 512, 4096, 1024, 512, 256
FLOPS = 2 * K * H * S + 2 * K * N * S + 2 * H * N * S

F32 = mybir.dt.float32
BF16 = mybir.dt.bfloat16
I32 = mybir.dt.int32
U32 = mybir.dt.uint32
U16 = mybir.dt.uint16
U8 = mybir.dt.uint8
FP8X4 = mybir.dt.float8_e4m3fn_x4
FP4X4 = mybir.dt.float4_e2m1fn_x4
RELU = mybir.ActivationFunctionType.Relu
COPY = mybir.ActivationFunctionType.Copy

P = 128
PACK = 4
SCALE_ROWS = K // 32
STAGE_FIRST = P - SCALE_ROWS
CHUNK = 128
CHUNKS = S // CHUNK
PAIR = 2
PAIRS = CHUNKS // PAIR
GATHER = 512
ROW_TILES = N // P
HIDDEN_BANKS = 5
W2_ROWS = 2
LATE = PAIR * CHUNK
VECTOR_GROUPS = (44, 82)


def tile_picked_lora_relu_p_kernel(
    tc, x_words, x_scales, w1_words, w1_scales, w2, w3_words, w3_scales, offs, out
):
    nc = tc.nc
    with ExitStack() as ctx:
        keep = ctx.enter_context(tc.tile_pool(name="keep", bufs=1))
        out_psum = ctx.enter_context(tc.psum_pool(name="out_psum", bufs=1))
        h_psum = ctx.enter_context(tc.psum_pool(name="h_psum", bufs=HIDDEN_BANKS))

        offsets = keep.tile([P, S // 16], U16, name="offsets")
        nc.sync.dma_start(offsets[:], offs)

        def load_scale_rows(plane, rows):
            for r in range(4):
                nc.sync.dma_start(plane[r:P:32, :].bitcast(I32), rows[r:SCALE_ROWS:4, :].bitcast(I32))

        scale_table = keep.tile([P, T], U8, name="scale_table", align_bytes=64)
        nc.scalar.dma_start(scale_table[P - SCALE_ROWS :, :].bitcast(I32), x_scales[0].bitcast(I32))

        x_table = keep.tile([P, T], U32, name="x_table", align_bytes=64)
        x_rows = x_words[0].rearrange("p c r -> p (c r)").bitcast(I32)
        nc.sync.dma_start(x_table[:, : T // 2].bitcast(I32), x_rows[:, : T // 2])
        w1_scale = keep.tile([P, N], U8, name="w1_scale", align_bytes=64)
        nc.vector.memset(w1_scale[:].bitcast(I32), 0)
        load_scale_rows(w1_scale[:], w1_scales[0])
        staged = keep.tile([P, LATE + N], U8, name="staged_scales", align_bytes=64)
        nc.sync.dma_start(staged[P - SCALE_ROWS :, LATE:].bitcast(I32), w3_scales[0].bitcast(I32))
        nc.sync.dma_start(x_table[:, T // 2 :].bitcast(I32), x_rows[:, T // 2 :])
        nc.vector.memset(scale_table[: P - SCALE_ROWS, :].bitcast(I32), 0)
        x_scale = keep.tile([P, S - LATE], U8, name="x_scale", align_bytes=64)
        nc.vector.memset(x_scale[:].bitcast(I32), 0)
        late_planes = keep.tile([P, LATE + N], U8, name="late_planes", align_bytes=64)
        nc.vector.memset(late_planes[:].bitcast(I32), 0)

        w2_rows = w2.rearrange("(p j) c -> p j c", j=PACK)
        w2_first = keep.tile([P, W2_ROWS, H], F32, name="w2_first", align_bytes=64)
        nc.sync.dma_start(w2_first[:], w2_rows[:, :W2_ROWS, :])
        w1_codes = keep.tile([P, 2 * N], U8, name="w1_codes", align_bytes=64)
        nc.sync.dma_start(w1_codes[:].bitcast(I32), w1_words[0].bitcast(I32))
        scale_picked = keep.tile([P, S - LATE], U8, name="scale_picked", align_bytes=64)
        nc.vector.tensor_copy(scale_picked[:], scale_table[:].indirect(offsets[:, : (S - LATE) // 16]))
        load_scale_rows(x_scale[:], scale_picked[P - SCALE_ROWS :, :])
        w2_last = keep.tile([P, W2_ROWS, H], F32, name="w2_last", align_bytes=64)
        nc.sync.dma_start(w2_last[:], w2_rows[:, W2_ROWS:, :])
        late_picked = keep.tile([P, T // 8], U8, name="late_picked", align_bytes=64)
        nc.vector.tensor_copy(late_picked[:], scale_table[:].indirect(offsets[:, (S - T // 8) // 16 :]))
        nc.vector.tensor_copy(staged[:, :LATE].bitcast(I32), late_picked[:, T // 8 - LATE :].bitcast(I32))
        load_scale_rows(late_planes[:], staged[P - SCALE_ROWS :, :])
        w3_codes = keep.tile([P, 2 * N], U8, name="w3_codes", align_bytes=64)
        nc.sync.dma_start(w3_codes[:].bitcast(I32), w3_words[0].bitcast(I32))
        w3_scale = late_planes[:, LATE:]

        w2_raw = [w2_first, w2_last]

        x_codes = []
        for g in range(S // GATHER):
            picked = keep.tile([P, GATHER], U32, name="x_codes%d" % g, align_bytes=64)
            columns = GATHER // 16
            nc.vector.tensor_copy(picked[:], x_table[:].indirect(offsets[:, g * columns : (g + 1) * columns]))
            x_codes.append(picked)

        def x_operand(first, count):
            g, at = divmod(first, GATHER)
            plane, place = (x_scale, first) if first < S - LATE else (late_planes, first - (S - LATE))
            return x_codes[g][:, at : at + count].bitcast(FP8X4), plane[:, place : place + count]

        def out_pass(target, row_tile, codes, plane, operand, start, stop):
            nc.tensor.matmul_mx(
                out=target,
                lhsT=codes[:, 2 * P * row_tile : 2 * P * (row_tile + 1)].bitcast(FP4X4),
                lhsT_scale=plane[:, P * row_tile : P * (row_tile + 1)],
                rhs=operand[0],
                rhs_scale=operand[1],
                start=start,
                stop=stop,
            )

        def pair_columns(c):
            return slice(c % PAIR * CHUNK, (c % PAIR + 1) * CHUNK)

        groups = {}

        def open_bank(bank, pair, row_tiles):
            for c in range(pair * PAIR, (pair + 1) * PAIR):
                for slot, row_tile in enumerate(row_tiles):
                    start = c % PAIR == 0 and slot == 0
                    operand = x_operand(c * CHUNK, CHUNK)
                    out_pass(bank[:, slot, pair_columns(c)], row_tile, w1_codes, w1_scale, operand, start, False)
                    groups[pair, row_tile] = (bank[:, slot, :], row_tile == row_tiles[-1])

        for pair, row_tiles in ((0, [0, 1]), (1, [0, 1]), (2, [0, 1])):
            bank = out_psum.tile([P, len(row_tiles), PAIR * CHUNK], F32, name="out_bank%d" % pair)
            open_bank(bank, pair, row_tiles)

        w2_codes = keep.tile([P, H], U32, name="w2_codes", align_bytes=64)
        w2_scale = keep.tile([P, H], U8, name="w2_scale", align_bytes=64)
        grouped = keep.tile([P, PACK, P, PACK], BF16, name="w2_grouped", align_bytes=64)

        def cast_views(part):
            src = w2_raw[part][:].rearrange("p j (m t) -> p m j t", t=PACK)
            dst = grouped[:, :, :, part * W2_ROWS : (part + 1) * W2_ROWS].rearrange("p t m j -> p m j t")
            return dst, src

        dst, src = cast_views(0)
        share = VECTOR_GROUPS[0]
        nc.scalar.activation(dst[:, share:], src[:, share:], COPY)
        nc.vector.tensor_copy(dst[:, :share], src[:, :share])
        dst, src = cast_views(1)
        share = VECTOR_GROUPS[1]
        for t in range(0, PACK, 2):
            nc.vector.tensor_copy(dst[:, :share, :, t : t + 2], src[:, :share, :, t : t + 2])
            nc.scalar.activation(dst[:, share:, :, t : t + 2], src[:, share:, :, t : t + 2], COPY)
        for t in range(PACK):
            cols = slice(t * P, (t + 1) * P)
            nc.vector.quantize_mx(
                out=w2_codes[:, cols].bitcast(FP8X4),
                scales=w2_scale[:, cols],
                in_=grouped[:, t, :, :].rearrange("p m j -> p (m j)"),
            )

        hidden = {}

        def hidden_tile(c, name):
            hidden[c] = keep.tile([P, CHUNK, PACK], BF16, name=name, align_bytes=64)

        def hidden_pass(bank, first, count, t):
            rhs, rhs_scale = x_operand(first, count)
            nc.tensor.matmul_mx(
                out=bank[:, t, :],
                lhsT=w2_codes[:, t * P : (t + 1) * P].bitcast(FP8X4),
                lhsT_scale=w2_scale[:, t * P : (t + 1) * P],
                rhs=rhs,
                rhs_scale=rhs_scale,
                start=True,
                stop=True,
            )

        def fill(first, count):
            bank = h_psum.tile([P, PACK, count], F32, name="h_bank")
            for t in reversed(range(PACK)):
                hidden_pass(bank, first, count, t)
            return bank

        def empty(bank, first, count, on_scalar):
            c, at = divmod(first, CHUNK)
            src = bank[:].rearrange("p t n -> p n t")
            if on_scalar:
                nc.scalar.activation(hidden[c][:, at : at + count, :], src, RELU)
            else:
                nc.vector.tensor_scalar_max(hidden[c][:, at : at + count, :], src, 0.0)

        quantised = {}

        def quantise(c):
            h_codes = keep.tile([P, CHUNK], U32, name="h_codes%d" % c, align_bytes=64)
            h_scale = keep.tile([P, CHUNK], U8, name="h_scale%d" % c, align_bytes=64)
            nc.vector.quantize_mx(
                out=h_codes[:].bitcast(FP8X4), scales=h_scale[:], in_=hidden[c][:].rearrange("p n t -> p (n t)")
            )
            quantised[c] = (h_codes[:].bitcast(FP8X4), h_scale[:])

        out_view = out.rearrange("(r p) s -> p r s", p=P)

        def second_product(c):
            for row_tile in range(ROW_TILES):
                target, closes = groups[c // PAIR, row_tile]
                stop = closes and c % PAIR == PAIR - 1
                out_pass(target[:, pair_columns(c)], row_tile, w3_codes, w3_scale, quantised[c], False, stop)

        def leave(pair, row_tile, on_scalar, name):
            columns = slice(pair * PAIR * CHUNK, (pair + 1) * PAIR * CHUNK)
            staged = keep.tile([P, PAIR * CHUNK], F32, name=name, align_bytes=64)
            if on_scalar:
                nc.scalar.copy(staged[:], groups[pair, row_tile][0])
            else:
                nc.vector.tensor_copy(staged[:], groups[pair, row_tile][0])
            nc.sync.dma_start(out_view[:, row_tile, columns], staged[:])

        banks = [h_psum.tile([P, PACK, CHUNK], F32, name="h_bank") for c in range(PAIR)]
        for t in range(PACK):
            for c in range(PAIR):
                hidden_pass(banks[c], c * CHUNK, CHUNK, t)
        for c in range(PAIR):
            hidden_tile(c, "h%d" % c)
            empty(banks[c], c * CHUNK, CHUNK, c == 0)
        def chunk(c, on_scalar):
            hidden_tile(c, "h%d" % c)
            empty(fill(c * CHUNK, CHUNK), c * CHUNK, CHUNK, on_scalar)

        chunk(2, True)
        chunk(3, False)
        for c in range(0, 3):
            quantise(c)
        chunk(4, True)
        chunk(5, False)
        for c in range(3, 6):
            quantise(c)
        chunk(6, True)
        second_product(0)
        second_product(1)
        leave(0, 0, True, "staged0_0")
        leave(0, 1, True, "staged0_1")
        half = CHUNK // 2
        last = (CHUNKS - 1) * CHUNK
        hidden_tile(7, "h7")
        empty(fill(last, half), last, half, False)
        empty(fill(last + half, half), last + half, half, True)
        quantise(6)
        quantise(7)
        second_product(2)
        second_product(3)
        leave(1, 0, True, "staged1_0")
        leave(1, 1, True, "staged1_1")
        both = h_psum.tile([P, ROW_TILES, CHUNK], F32, name="h_bank")
        for row_tile in range(ROW_TILES):
            out_pass(both[:, row_tile, :], row_tile, w1_codes, w1_scale, x_operand(6 * CHUNK, CHUNK), row_tile == 0, False)
        tail_banks = {}
        for row_tile in reversed(range(ROW_TILES)):
            tail_banks[row_tile] = h_psum.tile([P, CHUNK], F32, name="h_bank")
            out_pass(tail_banks[row_tile][:], row_tile, w1_codes, w1_scale, x_operand(last, CHUNK), True, False)
        second_product(4)
        second_product(5)
        leave(2, 0, False, "staged2_0")
        leave(2, 1, False, "staged2_1")
        tail = keep.tile([P, ROW_TILES, PAIR * CHUNK], F32, name="tail")
        for row_tile in range(ROW_TILES):
            out_pass(both[:, row_tile, :], row_tile, w3_codes, w3_scale, quantised[6], False, row_tile == 1)
        nc.scalar.copy(tail[:, :, :CHUNK], both[:])
        for row_tile in reversed(range(ROW_TILES)):
            out_pass(tail_banks[row_tile][:], row_tile, w3_codes, w3_scale, quantised[7], False, True)
        nc.vector.tensor_copy(tail[:, 1, CHUNK:], tail_banks[1][:])
        nc.scalar.copy(tail[:, 0, CHUNK:], tail_banks[0][:])
        nc.scalar.dma_start(out_view[:, 0, (CHUNKS - PAIR) * CHUNK :], tail[:, 0, :])
        nc.sync.dma_start(out_view[:, 1, (CHUNKS - PAIR) * CHUNK :], tail[:, 1, :])
